import numpy as np, ml_dtypes
CORES = [16,17,18,19,32,33,34,35]
N = 8
import mx_ref
BF = ml_dtypes.bfloat16
def gentries(a):
    return np.ascontiguousarray(a.reshape(8, 16, -1).transpose(0, 2, 1)).reshape(8, -1)
def gtable(e):
    e = np.asarray(e); return np.ascontiguousarray(e.reshape(8, -1, 16).transpose(0, 2, 1)).reshape(128, -1).astype(np.int32)
def gcols(t, e):
    v = np.concatenate([t.reshape(8, 16, -1, 4), np.zeros((8, 16, 1, 4), BF)], axis=2)
    return np.ascontiguousarray(np.stack([v[g][:, e[g]] for g in range(8)])).reshape(128, -1)
def tile(rs):
    return np.stack(rs, axis=2).reshape(128, -1).astype(BF)
def pick(q, e):
    c = np.concatenate([q[0].reshape(128, -1, 4), np.zeros((128, 1, 4), np.uint8)], axis=1); s = np.concatenate([q[1], np.ones((16, 1), np.uint8)], axis=1)
    return (np.ascontiguousarray(c[:, e].reshape(128, -1)), np.ascontiguousarray(s[:, e]))
def join(*qs):
    return (np.concatenate([q[0] for q in qs], axis=1), np.concatenate([q[1] for q in qs], axis=1))
def put(q, e, v):
    c, s = q[0].reshape(128, -1, 4).copy(), q[1].copy(); c[:, e] = v[0].reshape(128, -1, 4); s[:, e] = v[1]
    return (c.reshape(128, -1), s)
def pk(c, s):
    return (np.ascontiguousarray(c), mx_ref.live(s))
def emit(q):
    return q[0], q[1]
def packed(v, rng):
    q = [mx_ref.quantize(np.ascontiguousarray(v[r])) for r in range(N)]
    return np.stack([a for a, b in q]), np.stack([mx_ref.plane(b, rng) for a, b in q])
def values_of_codes():
    e, c = np.zeros((128, 128, 4), np.float32), np.zeros((128, 2, 4), np.uint8)
    e[np.arange(128), np.arange(128), 0] = 1
    c[:127, :, 0] = np.arange(256).reshape(2, 128).T[:127]
    return mx_ref.matmul(mx_ref.quantize(e.reshape(128, 512).astype(BF)), (c.reshape(128, 8), np.full((16, 2), 127, np.uint8))).T.reshape(-1).astype(np.float64)
CODE_VALUE, SCALE_VALUE = values_of_codes(), 2.0 ** (np.arange(256) - 127.0)
def decode(q):
    return (CODE_VALUE[q[0]].reshape(16, 8, -1, 4) * SCALE_VALUE[q[1]][:, None, :, None] + 0.0).reshape(128, -1).astype(np.float32)
def f(rng, *shape):
    return mx_ref.flush((rng.standard_normal(shape, dtype=np.float32) * np.exp2(rng.integers(-2, 3, shape[:-1] + (1,)))).astype(BF))
def wide(rng, *shape, cols=0):
    v = rng.standard_normal(shape, dtype=np.float32) * np.exp2(rng.integers(-12, 13, shape)).astype(np.float32)
    if cols: v *= np.repeat(np.exp2(rng.integers(-cols, cols + 1, shape[:-2] + (1, shape[-1] // 4))) * (rng.random(shape[:-2] + (1, shape[-1] // 4)) > 0.0625), 4, axis=-1).astype(np.float32)
    return mx_ref.flush(v.astype(BF))
C, H = 320, 160
STEP = [1, 2, 4]
def numbers_of(rng):
    return {"x": np.array(f(rng, N, 128, 4 * C)), "u": np.array(f(rng, N, 128, 512)), "v": np.array(f(rng, N, 128, 512))}
def stored(m):
    return {"ml": np.stack([gtable(m[r]) for r in range(N)])}
def paired(e):
    m = np.zeros_like(e)
    np.put_along_axis(m, e, np.roll(e, H, axis=-1), axis=-1)
    return m
def pairings(rng):
    return paired(rng.permuted(np.tile(np.arange(C), (N, 8, 1)), axis=2))
def zigzag(rng, loop):
    s, t = rng.permutation(H), rng.permutation(H)
    a = np.concatenate([np.roll(t, -1), H + np.roll(s, -1)]).reshape(-1, 2)
    if not loop: a[H // 2 - 1, 1], a[-1, 0] = int(a[-1, 0]), int(a[H // 2 - 1, 1])
    b = np.concatenate([s, H + t]).reshape(-1, 2)
    return [paired(np.concatenate([k[:, 0], k[:, 1]])) for k in (a, b)]
def coil(rng):
    s = rng.permutation(H)
    k = np.concatenate([s, H + np.roll(s[:-1], -1), H + s[-1:]]).reshape(-1, 2)
    k[H // 2 - 1, 1], k[-1, 0] = int(k[-1, 0]), int(k[H // 2 - 1, 1])
    return paired(np.concatenate([k[:, 0], k[:, 1]]))
def layers(rng, still=[], pairs=False):
    w = np.array(f(rng, N, 128, 2048)).reshape(N, 8, 16, 4, 8, 16, 4)
    for i in still:
        w[:, :, i] = 0
        w[:, :, :, :, :, i] = 0
    if pairs:
        w[:, :, :, :, :, 8:] = 0
        for g in range(8):
            w[:, g, 8, 0, g, 8, 0] = -28.0
            for b in range(4): w[:, g, 10, b, g, 9, 0] = -2.0 ** (b - 5)
    return w
def weights(rng, w):
    c, s = packed(np.ascontiguousarray(w).reshape(N, 128, 2048), rng)
    return {"wc": c, "ws": s}
def setup_inputs(rng):
    return {**numbers_of(rng), **stored(pairings(rng)), **weights(rng, layers(rng))}
def setup_inputs_ties(rng):
    d = numbers_of(rng)
    o = rng.permutation(N)
    k = rng.integers(0, 4, (N, 8, C))
    k[o[0]] = 0
    k[o[1]] -= 4
    k[o[2]] = np.arange(C) < H
    kind = rng.permutation(8)
    m = np.zeros((N, 8, C), np.int64)
    for g in range(8):
        if 4 <= kind[g] < 7: k[:, g] = np.sort(k[:, g].reshape(N, 2, H), axis=1).reshape(N, C)
        for r in range(N):
            p, q = r ^ STEP[0], r ^ STEP[1]
            if kind[g] < 4 and r < p:
                a = zigzag(rng, kind[g] == 3)
                j = int(rng.integers(2))
                m[r, g], m[p, g] = a[j], a[1 - j]
            if 4 <= kind[g] < 6 and r < min(p, q, p ^ STEP[1]):
                m[r, g], m[q, g] = zigzag(rng, False)
                m[p, g] = m[p ^ STEP[1], g] = paired(np.arange(C))
            if kind[g] == 7: m[r, g] = paired(np.concatenate([rng.permutation(H), H + rng.permutation(H)]))
        if kind[g] == 6:
            m[:, g] = paired(np.arange(C))
            r = int(rng.integers(N))
            if STEP[0] ^ STEP[1] == STEP[2]: m[r, g] = coil(rng)
            else: m[r, g], m[r ^ STEP[2], g] = zigzag(rng, False)
    x = d["x"].reshape(N, 8, 16, C, 4)
    x[:, :, 0] = 0
    x[:, :, 0, :, 0] = k.astype(np.float32).astype(BF)
    a = np.exp2(rng.integers(-3, 4, (N, 8, 1)).astype(np.float32))
    x[:, :, 8:] = 0
    x[:, :, 8, :, 0] = (-1.125 * a).astype(BF)
    x[:, :, 10, :, 0] = (-0.0703125 * a).astype(BF)
    u = d["u"].reshape(N, 128, 128, 4)
    u[:, :, ::16] = 0
    for h in range(0, 128, 16): u[:, h, h, 0] = 1.0
    return {"x": x.reshape(N, 128, 4 * C), "u": u.reshape(N, 128, 512), "v": d["v"], **stored(twist(k, m)), **weights(rng, layers(rng, [0], True))}
def setup_inputs_near(rng):
    d = numbers_of(rng)
    x = d["x"].astype(np.float32).reshape(N, 8, 16, C, 4)
    x[:, :, 0] = 0
    x[:, :, 8:] = 0
    u = d["u"].reshape(N, 128, 128, 4)
    u[:, :, ::16] = 0
    w = layers(rng, [0, 8, 9, 10, 11, 12, 13, 14, 15])
    o = rng.permutation(N) % 4
    for r in range(N):
        c = rng.choice([-1.0, 1.0], (8, 1))
        s = rng.integers(0, 16, (8, C))
        digits = ((s[:, :, None] >> np.arange(4)) & 1) * np.exp2(np.arange(4) - 23.0)
        if o[r] < 2:
            x[r, :, 0, :, 0] = c
            x[r, :, 8] = digits
            x[r, :, 11, :, 0] = 2.0 ** -10
        elif o[r] == 2: x[r, :, 8] = digits * rng.choice([-1.0, 1.0], (8, C, 1))
        else:
            x[r, :, 8, :, 0] = np.where(s < 8, 1.25, 0.0) * 2.0 ** -30 * c
            x[r, :, 9, :, 0] = np.where(s < 8, 0.0, 1.125) * 2.0 ** -30 * c
            for g in rng.permutation(8)[:4]:
                e = rng.choice([-1.0, 1.0], C) * 2.0 ** -30
                x[r, g, 8, :, 0] = 1.25 * e
                x[r, g, 9, :, 0] = -1.125 * e
            for g in range(8):
                w[r, g, 8, 0, g, 12, 0] = 2.0 ** -8
                w[r, g, 8, 0, g, 14, 0] = 64.0
                w[r, g, 1, 0, g, 2, 0] = 256.0
        at = [0, C - 1, int(rng.integers(C)), int(rng.integers(C))]
        for g, j in zip(rng.permutation(8)[:4], at): x[r, g, 0, j, 0] = 2.0 ** 29 * rng.choice([-1.0, 1.0])
        k = 1.0 if o[r] == 0 else 2.0 ** -30
        for h in range(0, 128, 16):
            u[r, h, h, 0] = k if o[r] < 2 else 1.0
            if o[r] < 2: u[r, h + 11, h, 0] = k
            if o[r] < 3: u[r, h + 8, h] = k
            else:
                u[r, h + 8, h, 0] = k
                u[r, h + 9, h, 0] = 1.125 * k
                u[r, h + 12, h, 0] = k
    return {"x": x.reshape(N, 128, 4 * C).astype(BF), "u": u.reshape(N, 128, 512), "v": d["v"], **stored(pairings(rng)), **weights(rng, w)}
def setup_inputs_odd(rng):
    d = numbers_of(rng)
    x = (1.0 + (2 * rng.integers(0, 64, (N, 16, 8, C, 4)) + 1) * 2.0 ** -7) * np.exp2(-rng.integers(0, 7, (N, 16, 8, C, 4)).astype(np.float64)) * rng.choice([-1.0, 1.0], (N, 16, 8, C, 4))
    x[:, :, 0, :, 0] = 1.96875 * 2.0 ** 8 * rng.choice([-1.0, 1.0], (N, 16, C))
    u = d["u"].reshape(N, 16, 8, 128, 4)
    u[:, :, 0, ::16] = 0
    for r in range(N):
        for i, g in enumerate(rng.permutation(8)[:4]):
            x[r, 2 * g, 1, :, 0] = (8 + rng.integers(0, 2, C)) * 2.0 ** (i - 8)
            u[r, :, :, 16 * g] = 0
            u[r, 2 * g, 1, 16 * g, 0] = 1.0
    return {"x": x.astype(np.float32).reshape(N, 128, 4 * C).astype(BF), "u": u.reshape(N, 128, 512), "v": d["v"], **stored(pairings(rng)), **weights(rng, layers(rng, [0, 8]))}
def setup_inputs_ends(rng):
    d = numbers_of(rng)
    x = np.zeros((N, 8, 16, C, 4))
    u = d["u"].astype(np.float32).reshape(N, 128, 128, 4)
    v = d["v"].astype(np.float32)
    w = np.zeros((N, 128, 4, 128, 4), np.float32)
    m = pairings(rng)
    o, e = rng.permutation(N) % 4, rng.permutation(N) % 4
    i = np.arange(128)
    for r in range(N):
        h = rng.permutation(8)
        c = np.where(h < 2, 0.0, h % 2 * 2.0 - 1.0)[None, :, None]
        k = np.array([2.0, 4.0, -4.0])[rng.permutation(8) % 3]
        low = -(0.9 + 0.1 * rng.random((8, 16, C, 4))) * 2.0 ** 28
        if o[r] == 0: x[r] = low
        if o[r] == 1: x[r] = low * rng.choice([-1.0, 1.0], (C, 1))
        if o[r] < 2:
            u[r, :, ::16] = c * (0.9 + 0.1 * rng.random((128, 8, 4))) * 2.0 ** 30
            v[r] = rng.choice([-1.0, 1.0], (128, 512)) * (0.9 + 0.1 * rng.random((128, 512))) * 2.0 ** 30
        if o[r] == 2:
            x[r] = -(1.0 + 0.125 * rng.integers(0, 8, (8, 16, C, 4))) * 2.0 ** -30
            u[r, :, ::16] = c * (1.0 + 0.125 * rng.integers(0, 8, (128, 8, 4))) * 2.0 ** -30
            v[r] = rng.choice([-1.0, 1.0], (128, 512)) * (1.0 + 0.125 * rng.integers(0, 8, (128, 512))) * 2.0 ** -30
            k[:] = 32.0
        if o[r] == 3:
            x[r] = d["x"][r].astype(np.float32).reshape(8, 16, C, 4)[:, :, :1]
            u[r, :, ::16] *= np.abs(c).astype(np.float32)
        for b in range(4): w[r, i, b, i, b] = k[i // 16]
        if e[r] < 3: m[r] = [paired(np.arange(C)), np.arange(C) ^ 1, C - 1 - np.arange(C)][e[r]]
    return {"x": x.astype(np.float32).reshape(N, 128, 4 * C).astype(BF), "u": u.reshape(N, 128, 512).astype(BF), "v": v.astype(BF), **stored(m), **weights(rng, w.astype(BF))}
def setup_inputs_spread(rng):
    d = setup_inputs(rng)
    d["x"] = wide(rng, N, 128, 4 * C, cols=6)
    return d
def check_inputs(d):
    b = []
    for k in ("x", "u", "v"):
        a = np.abs(d[k].astype(np.float32))
        if not (np.isfinite(a).all() and ((a == 0) | (a >= 2.0 ** -30) & (a <= 2.0 ** 30)).all()): b.append("a value of " + k)
    none, least, most = [emit(mx_ref.quantize(np.full((128, 16), k, np.float32).astype(BF)))[1][0, 0] for k in (0.0, 2.0 ** -8, 2.0 ** 8)]
    for r in range(N):
        e = gentries(d["ml"][r]).astype(np.int64)
        if not ((e >= 0) & (e < C)).all(): b.append("an entry of ml")
        elif (e == np.arange(C)).any() or (np.take_along_axis(e, e, axis=1) != np.arange(C)).any(): b.append("ml: not a pairing")
        if ((d["wc"][r] == 0x7F) | (d["wc"][r] == 0xFF)).any(): b.append("wc: a code that is no number")
        s = mx_ref.live(d["ws"][r])
        if ((s != none) & ((s < least) | (s > most))).any(): b.append("ws: a scale out of range")
    return b
def twist(s, m):
    e = np.zeros(m.shape, np.int64) + np.arange(C)
    swap = H * (s[..., :H] > s[..., H:])
    e[..., :H] += swap
    e[..., H:] -= swap
    return np.take_along_axis(e, np.take_along_axis(m, e, axis=-1), axis=-1)
def glued(a, b):
    at = np.tile(np.arange(C), (8, 1))
    far = at >= H
    done = np.zeros((8, C), bool)
    for _ in range(H + 1):
        at = np.where(done, at, np.where(far, np.take_along_axis(b, at, axis=1), np.take_along_axis(a, at, axis=1)))
        done = done | ((at >= H) == far)
        at = np.where(done, at, np.where(far, at + H, at - H))
        far = far ^ ~done
        if done.all(): break
    return at
def plus(s, t):
    return (s.astype(np.float32) + t.astype(np.float32)).astype(BF)
def reference(x, u, v, ml, wc, ws):
    qu = [mx_ref.quantize(u[r]) for r in range(N)]
    lay = [pk(wc[r], ws[r]) for r in range(N)]
    now = [x[r] for r in range(N)]
    mate = [gentries(ml[r]).astype(np.int64) for r in range(N)]
    for step in STEP:
        turned, qa = [], []
        for r in range(N):
            s = mx_ref.matmul(qu[r], mx_ref.quantize(now[r]))[::16] + np.float32(0.0)
            turned.append(twist(s, mate[r]))
            qz = mx_ref.quantize(plus(now[r], gcols(now[r], turned[r])))
            qa.append(mx_ref.quantize(tile([mx_ref.matmul(pick(lay[r], np.arange(128 * b, 128 * b + 128)), qz) * np.float32(0.015625) for b in range(4)])))
        made = []
        for r in range(N):
            p = r ^ step
            mate[r] = glued(turned[r], turned[p])
            t = decode(join(pick(qa[r], np.arange(H)), pick(qa[p], np.arange(H, C)))).astype(BF)
            made.append(plus(now[r], gcols(t, mate[r])))
        now = made
    y, mo = np.zeros((N, 128, C), np.float32), np.zeros((N, 8, C), np.float32)
    oc, osc = np.zeros((N, 128, 4 * C), np.uint8), np.zeros((N, 16, C), np.uint8)
    for r in range(N):
        q = mx_ref.quantize(now[r])
        y[r] = mx_ref.matmul(mx_ref.quantize(v[r]), q)
        mo[r] = mate[r]
        oc[r], osc[r] = emit(q)
    return {"y": y, "mo": mo, "oc": oc, "osc": osc}

@@ -1,0 +1,460 @@
+from concourse.mybir import dt, AluOpType, ActivationFunctionType
+
+BF, F32, I32, U16, U8, MX = "bfloat16", "float32", "int32", "uint16", "uint8", "float8_e4m3fn_x4"
+STEP = [1, 2, 4]
+C, H = 320, 160
+LOW = 256
+WIN = LOW + H
+CODES = WIN + H
+
+SCRATCH = {
+    "x0": ("sbuf", [128, 4 * C], BF), "x1": ("sbuf", [128, 4 * C], BF), "x2": ("sbuf", [128, 4 * C], BF), "x3": ("sbuf", [128, 4 * C], BF),
+    "z": ("sbuf", [128, 4 * C], BF), "a": ("sbuf", [128, 4 * C], BF),
+    "et": ("sbuf", [128, 528], BF), "eo": ("sbuf", [128, 528], BF), "eq": ("sbuf", [128, 512], MX), "eqs": ("sbuf", [128, 512], U8),
+    "ut": ("sbuf", [128, 512], BF), "uq": ("sbuf", [128, 128], MX), "uqs": ("sbuf", [128, 128], U8),
+    "u2": ("sbuf", [128, 128], MX), "u2s": ("sbuf", [128, 128], U8),
+    "vt": ("sbuf", [128, 512], BF), "vq": ("sbuf", [128, 128], MX), "vqs": ("sbuf", [128, 128], U8),
+    "wq": ("sbuf", [128, 512], MX), "wqs": ("sbuf", [128, 512], U8),
+    "qx": ("sbuf", [128, C], MX), "qxs": ("sbuf", [128, C], U8),
+    "qz": ("sbuf", [128, C], MX), "qzs": ("sbuf", [128, C], U8),
+    "qu": ("sbuf", [128, H], MX), "qus": ("sbuf", [128, H], U8),
+    "ps": ("psum", [128, 4096], F32),
+    "slo": ("sbuf", [128, H], F32), "sw": ("sbuf", [128, C], BF), "gs": ("sbuf", [128, C], BF), "sc": ("sbuf", [128, H + C], BF),
+    "mli": ("sbuf", [128, 20], I32), "zf": ("sbuf", [128, 20], F32), "wk": ("sbuf", [128, 20], F32), "kf": ("sbuf", [128, 20], F32),
+    "kb": ("sbuf", [128, 20], F32), "mm": ("sbuf", [128, 20], U16), "cc": ("sbuf", [128, 30], F32), "kc": ("sbuf", [128, 40], F32),
+    "pq": ("sbuf", [128, 40], F32), "nf": ("sbuf", [128, 20], F32),
+    "mlp": ("sbuf", [128, 20], I32), "pzf": ("sbuf", [128, 20], F32), "pkb": ("sbuf", [128, 20], F32),
+    "bits": ("sbuf", [128, 30], F32), "bitp": ("sbuf", [128, 30], F32),
+    "ident": ("sbuf", [128, WIN], F32), "aown": ("sbuf", [128, WIN], F32), "wa": ("sbuf", [128, CODES], F32), "wb": ("sbuf", [128, CODES], F32),
+    "su": ("sbuf", [128, H], F32), "ssu": ("sbuf", [128, H], F32), "stu": ("sbuf", [128, 10], U16),
+    "cf": ("sbuf", [128, C], F32), "csc": ("sbuf", [128, C], F32), "zo": ("sbuf", [128, 20], U16),
+    "fin": ("sbuf", [128, C], F32), "mof": ("sbuf", [128, C], F32), "yb": ("sbuf", [128, C], F32),
+    "d0": ("sbuf", [128, C], F32), "ds": ("sbuf", [128, 16], F32), "d1": ("sbuf", [128, 16], F32), "d2": ("sbuf", [128, 16], F32), "tcol": ("sbuf", [128, 16], F32),
+    "pix": ("sbuf", [128, 20], I32), "qi": ("sbuf", [128, 20], I32), "qo": ("sbuf", [128, 20], U16), "qf": ("sbuf", [128, 1], F32), "q1": ("sbuf", [128, 1], F32),
+    "e0": ("sbuf", [128, H], BF), "es": ("sbuf", [128, 16], F32), "e1": ("sbuf", [128, 16], F32), "e2": ("sbuf", [128, 16], F32),
+    "bias": ("sbuf", [128, 1], F32), "bb": ("sbuf", [128, 1], F32), "bm": ("sbuf", [128, 1], F32), "bz": ("sbuf", [128, 1], F32),
+    "uli": ("sbuf", [128, 8], I32), "ul": ("sbuf", [128, 8], U16),
+}
+for _b in range(4):
+    SCRATCH["xp%d" % _b] = ("sbuf", [128, WIN], BF)
+    SCRATCH["b%d" % _b] = ("sbuf", [128, C], F32)
+for _r in range(3):
+    SCRATCH["scn%d" % _r] = ("sbuf", [128, H], F32)
+    SCRATCH["lu%d" % _r] = ("sbuf", [128, 10], U16)
+    SCRATCH["nl%d" % _r] = ("sbuf", [128, 20], U16)
+    SCRATCH["np%d" % _r] = ("sbuf", [128, 20], U16)
+    SCRATCH["ql%d" % _r] = ("sbuf", [128, H], MX)
+    SCRATCH["qls%d" % _r] = ("sbuf", [128, H], U8)
+    SCRATCH["pl%d" % _r] = ("sbuf", [128, H], MX)
+    SCRATCH["pls%d" % _r] = ("sbuf", [128, H], U8)
+SEMAPHORES = ["sv", "ss", "st", "sg", "sent", "outs", "ldxl", "ldxu", "ldu", "ldm", "ldw", "ldws", "ldv", "arrm"]
+for _r in range(3):
+    SEMAPHORES += ["arrl%d" % _r, "arrc%d" % _r]
+
+LO, UP = (H, C), (0, H)
+
+
+def rank_program(g, core, T, topo):
+    rank = T.rank_of(core)
+    if rank is None:
+        return
+    queues = {"v": g.vector, "s": g.scalar, "t": g.tensor, "g": g, "y": g.sync}
+    home = {"v": "sv", "s": "ss", "t": "st", "g": "sg"}
+    count = {}
+    known = {q: {} for q in queues}
+    snap = {}
+    log = {}
+
+    def meets(e, r):
+        return e[0] < r[2] and r[1] < e[1] and (e[2] is None or r[3] is None or e[2] == r[3])
+
+    def full(r):
+        return (r[0], r[1], r[2], r[3] if len(r) > 3 else None)
+
+    def hold(q, need):
+        while need:
+            best = None
+            for s, v in sorted(need):
+                covers = sum(1 for s2, v2 in need if snap[(s, v)].get(s2, 0) >= v2)
+                if best is None or covers > best[0]: best = (covers, s, v)
+            _, s, v = best
+            queues[q].wait_ge(T.sem[s], v)
+            for s2, v2 in snap[(s, v)].items():
+                if known[q].get(s2, 0) < v2: known[q][s2] = v2
+            need = [(s2, v2) for s2, v2 in need if known[q].get(s2, 0) < v2]
+
+    def waits(q, reads, writes):
+        need = set()
+        for r in reads:
+            for e in log.get(r[0], []):
+                if e[6] and meets(e, r): need.add((e[3], e[4]))
+        for r in writes:
+            for e in log.get(r[0], []):
+                if meets(e, r) and (e[6] or e[5] != q): need.add((e[3], e[4]))
+        hold(q, [(s, v) for s, v in need if known[q].get(s, 0) < v])
+
+    def record(q, reads, writes, s, v):
+        for r in writes:
+            log[r[0]] = [e for e in log.get(r[0], []) if not (r[1] <= e[0] and e[1] <= r[2] and (r[3] is None or r[3] == e[2]))]
+            log[r[0]].append((r[1], r[2], r[3], s, v, q, True))
+        for r in reads:
+            log.setdefault(r[0], []).append((r[1], r[2], r[3], s, v, q, False))
+
+    def do(q, call, reads, writes, sem=None):
+        reads, writes = [full(r) for r in reads], [full(r) for r in writes]
+        waits(q, reads, writes)
+        inc = 16 if sem else 1
+        s = sem or home[q]
+        call(queues[q]).then_inc(T.sem[s], inc)
+        count[s] = count.get(s, 0) + inc
+        snap[(s, count[s])] = dict(known[q])
+        snap[(s, count[s])][s] = count[s]
+        record(q, reads, writes, s, count[s])
+
+    def send(dst, engines, pairs, sem):
+        rid, pid, _ = topo.addr(dst)
+        m = sum(1 << e for e in engines)
+        for src, land, region in pairs:
+            waits("g", [full(region)], [])
+            g.remote_dma(land, src, T.sem[sem], T.sem.sent, pid, rid, m)
+            count["sent"] = count.get("sent", 0) + len(engines)
+
+    def arrival(regions, sem, n):
+        count[sem] = n
+        snap[(sem, n)] = {sem: n}
+        record("remote", [], [full(r) for r in regions], sem, n)
+
+    op = AluOpType
+    COPY = ActivationFunctionType.Copy
+
+    def cols(name, a, b):
+        return T[name][:, a:b]
+
+    def tt(out, in0, in1, o, reads, writes):
+        do("v", lambda q: q.tensor_tensor(out, in0, in1, o), reads, writes)
+
+    def ts(out, in0, s1, s2, o1, o2, reads, writes):
+        if o2 is None:
+            do("v", lambda q: q.tensor_scalar(out, in0, s1, None, o1), reads, writes)
+        else:
+            do("v", lambda q: q.tensor_scalar(out, in0, s1, s2, o1, o2), reads, writes)
+
+    def vcopy(out, in_, reads, writes):
+        do("v", lambda q: q.tensor_copy(out, in_), reads, writes)
+
+    def scopy(out, in_, reads, writes, scale=1.0):
+        if scale == 1.0: do("s", lambda q: q.activation(out, in_, COPY), reads, writes)
+        else: do("s", lambda q: q.activation(out, in_, COPY, scale=scale), reads, writes)
+
+    def pick(q, out, oreg, win, wn, off, a):
+        f = vcopy if q == "v" else scopy
+        f(out, T[win][:, 0:wn].indirect(T[off][:, a:a + 10]), [(win, 0, wn), (off, a, a + 10)], [oreg])
+
+    def scan(out, oreg, src, a, n):
+        do("v", lambda q: q.tensor_tensor_scan(out, T.d0[:, 0:n], T[src][:, a:a + n], 0.0, op.add, op.min), [("d0", 0, C), (src, a, a + n)], [oreg])
+
+    def scan_bits(a, src, b):
+        do("v", lambda q: q.tensor_tensor_scan(cols("sc", a, a + H), T.e0[:], T[src][:, b:b + H], 0.0, op.add, op.min), [("e0", 0, H), (src, b, b + H)], [("sc", a, a + H)])
+
+    def pick2(name, o, win, wn, off, a):
+        for q, c, d in (("v", 0, 6), ("s", 6, 10)):
+            f = vcopy if q == "v" else scopy
+            f(cols(name, o + 16 * c, o + 16 * d), T[win][:, 0:wn].indirect(T[off][:, a + c:a + d]), [(win, 0, wn), (off, a + c, a + d)], [(name, o + 16 * c, o + 16 * d)])
+
+    def entries(out, oreg, src, a, n, col):
+        ts(out, T[src][:, a + 15:a + n:16], T[col][:, 0:1], None, op.add, None, [(src, a, a + n), (col, 0, 1)], [oreg])
+
+    def quant(out, scales, tile, a, n, dst=0):
+        do("v", lambda q: q.quantize_mx(T[out][:, dst:dst + n], T[scales][:, dst:dst + n], T[tile][:, 4 * a:4 * (a + n)]),
+           [(tile, a, a + n)], [(out, dst, dst + n), (scales, dst, dst + n)])
+
+    def psum(bank, n):
+        return T.ps[:, 512 * bank:512 * bank + n]
+
+    def product(bank, w, ws, wa, x, xs, a, n):
+        do("t", lambda q: q.matmul_mx(psum(bank, n), T[w][:, wa:wa + 128], T[ws][:, wa:wa + 128], T[x][:, a:a + n], T[xs][:, a:a + n], True, True),
+           [(w, wa, wa + 128), (ws, wa, wa + 128), (x, a, a + n), (xs, a, a + n)], [("bank%d" % bank, 0, 512)])
+
+    def evacuate(q, out, oreg, bank, scale=1.0):
+        if q == "s": scopy(out, psum(bank, H), [("bank%d" % bank, 0, 512)], [oreg], scale)
+        else: ts(out, psum(bank, H), scale, None, op.mult, None, [("bank%d" % bank, 0, 512)], [oreg])
+
+    def load(q, out, in_, region, sem):
+        do(q, lambda e: e.dma_start(out, in_), [], [region], sem)
+
+    load("y", cols("x0", 4 * H, 4 * C), T.x[:, 4 * H:4 * C], ("x0", H, C), "ldxl")
+    load("s", T.mli[:], T.ml[:], ("mli", 0, 20), "ldm")
+    load("y", cols("x0", 0, 4 * H), T.x[:, 0:4 * H], ("x0", 0, H), "ldxu")
+    load("s", T.ut[:], T.u[:], ("ut", 0, 128), "ldu")
+    load("y", T.wq[:].bitcast(dt.uint8), T.wc[:], ("wq", 0, 512), "ldw")
+    load("s", T.wqs[:], T.ws[:], ("wqs", 0, 512), "ldws")
+    load("y", T.vt[:], T.v[:], ("vt", 0, 128), "ldv")
+
+    do("v", lambda q: q.memset(T.eo[:], 1.0), [], [("eo", 0, 528)])
+    do("g", lambda q: q.iota(T.pix[:], [[0, 20]], 0, 1), [], [("pix", 0, 20)])
+    do("g", lambda q: q.iota(T.tcol[:], [[1, 16]], 0, 0, allow_small_or_imprecise_dtypes=True), [], [("tcol", 0, 16)])
+    do("g", lambda q: q.affine_select(T.et[:], T.eo[:], [[-1, 528]], op.is_equal, 0.0, 3, 4), [("eo", 0, 528)], [("et", 0, 528)])
+    do("g", lambda q: q.iota(T.uli[:], [[16, 8]], 0, 0), [], [("uli", 0, 8)])
+    do("g", lambda q: q.iota(T.ident[:], [[1, WIN]], 0, 0, allow_small_or_imprecise_dtypes=True), [], [("ident", 0, WIN)])
+    first = T.cores[rank ^ STEP[0]]
+    lanes = topo.engines(core, first)[:8]
+    arrival([("mlp", 0, 20)], "arrm", len(lanes))
+    arrival([("bitp", 0, 30)], "arrl0", len(lanes))
+    send(first, lanes, [(T.mli[:], T.mlp[:], ("mli", 0, 20))], "arrm")
+    do("v", lambda q: q.tensor_scalar(T.qi[:], T.pix[:], 15, None, op.bitwise_and), [("pix", 0, 20)], [("qi", 0, 20)])
+    vcopy(T.qf[:], cols("qi", 0, 1), [("qi", 0, 1)], [("qf", 0, 1)])
+    vcopy(T.qo[:], T.qi[:], [("qi", 0, 20)], [("qo", 0, 20)])
+    ts(T.q1[:], T.qf[:], 1.0, None, op.add, None, [("qf", 0, 1)], [("q1", 0, 1)])
+    ts(T.d2[:], T.tcol[:], T.qf[:, 0:1], 4096.0, op.is_equal, op.mult, [("tcol", 0, 16), ("qf", 0, 1)], [("d2", 0, 16)])
+    ts(T.d1[:], T.tcol[:], T.q1[:, 0:1], -1024.0, op.is_equal, op.mult, [("tcol", 0, 16), ("q1", 0, 1)], [("d1", 0, 16)])
+    tt(T.ds[:], T.d2[:], T.d1[:], op.add, [("d2", 0, 16), ("d1", 0, 16)], [("ds", 0, 16)])
+    scopy(T.d0[:], T.ds[:].indirect(T.qo[:, 0:20]), [("ds", 0, 16), ("qo", 0, 20)], [("d0", 0, C)])
+    ts(T.bias[:], T.qf[:], 14.5, 1024.0, op.is_lt, op.mult, [("qf", 0, 1)], [("bias", 0, 1)])
+    ts(T.e2[:], T.tcol[:], T.qf[:, 0:1], 8.0, op.is_equal, op.mult, [("tcol", 0, 16), ("qf", 0, 1)], [("e2", 0, 16)])
+    ts(T.e1[:], T.tcol[:], T.q1[:, 0:1], -2.0, op.is_equal, op.mult, [("tcol", 0, 16), ("q1", 0, 1)], [("e1", 0, 16)])
+    ts(T.bb[:], T.qf[:], 14.5, 2.0, op.is_lt, op.mult, [("qf", 0, 1)], [("bb", 0, 1)])
+    tt(T.es[:], T.e2[:], T.e1[:], op.add, [("e2", 0, 16), ("e1", 0, 16)], [("es", 0, 16)])
+    scopy(T.e0[:], T.es[:].indirect(T.qo[:, 0:10]), [("es", 0, 16), ("qo", 0, 10)], [("e0", 0, H)])
+    ts(T.bm[:], T.bb[:], -1.0, None, op.add, None, [("bb", 0, 1)], [("bm", 0, 1)])
+    ts(T.bz[:], T.bias[:], -float(LOW), None, op.add, None, [("bias", 0, 1)], [("bz", 0, 1)])
+    vcopy(T.ul[:], T.uli[:], [("uli", 0, 8)], [("ul", 0, 8)])
+    for b in range(4):
+        do("v", lambda q: q.memset(cols("xp%d" % b, H, LOW), 0.0), [], [("xp%d" % b, H, LOW)])
+
+    def unit(b):
+        do("v", lambda q: q.quantize_mx(cols("eq", 128 * b, 128 * b + 128), cols("eqs", 128 * b, 128 * b + 128), cols("et", 3 - b, 515 - b)),
+           [("et", 0, 528)], [("eq", 128 * b, 128 * b + 128), ("eqs", 128 * b, 128 * b + 128)])
+
+    def scores(half):
+        product(0 if half == LO else 4, "u2", "u2s", 0, "qx", "qxs", half[0], H)
+
+    def state_quant(x, half):
+        quant("qx", "qxs", x, half[0], H, half[0])
+
+    def address(half):
+        return (LOW, WIN) if half == LO else (0, H)
+
+    def plane(x, b, half):
+        a, e = address(half)
+        scopy(cols("xp%d" % b, a, e), T[x][:, 4 * half[0] + b:4 * half[1]:4], [(x, half[0], half[1], b)], [("xp%d" % b, a, e)])
+
+    def scores_low_out():
+        evacuate("s", T.slo[:], ("slo", 0, H), 0)
+
+    def prepare(zf="zf", kb="kb"):
+        return [lambda: ts(T.wk[:], T[zf][:], H - 0.5, -float(H), op.is_gt, op.mult, [(zf, 0, 20)], [("wk", 0, 20)]),
+                lambda: tt(T.kf[:], T[zf][:], T.wk[:], op.add, [(zf, 0, 20), ("wk", 0, 20)], [("kf", 0, 20)]),
+                lambda: ts(T[kb][:], T.kf[:], 1.0 / LOW, T.bb[:, 0:1], op.mult, op.add, [("kf", 0, 20), ("bb", 0, 1)], [(kb, 0, 20)])]
+
+    def choose(bits, a, step):
+        for k, col, f in ((10, "bm", 4.0), (20, "bb", -4.0), (0, "bb", -4.0)):
+            ts(cols("cc", k, k + 10), T[bits][:, a:10 * step:step], T[col][:, 0:1], f, op.add, op.mult,
+               [(bits, 0, 10 * step), (col, 0, 1)], [("cc", k, k + 10)])
+
+    def blend(kb):
+        for k in (10, 0):
+            tt(cols("kc", 2 * k, 2 * k + 20), cols("cc", k, k + 20), T[kb][:], op.add, [("cc", k, k + 20), (kb, 0, 20)], [("kc", 2 * k, 2 * k + 20)])
+
+    def turn(bits, a, step, out):
+        n = 10 * step
+        for k in (20, 0):
+            tt(cols("pq", k, k + 20), T[bits][:, n + a:3 * n:step], cols("kc", k, k + 20), op.add, [(bits, n, 3 * n), ("kc", k, k + 20)], [("pq", k, k + 20)])
+        for k in (20, 0):
+            tt(cols("nf", k // 2, k // 2 + 10), cols("pq", k, k + 10), cols("pq", k + 10, k + 20), op.max, [("pq", k, k + 20)], [("nf", k // 2, k // 2 + 10)])
+        for k in (10, 0):
+            ts(cols(out, k, k + 10), cols("nf", k, k + 10), float(LOW), None, op.mult, None, [("nf", k, k + 10)], [(out, k, k + 10)])
+
+    vcopy(T.zf[:], T.mli[:], [("mli", 0, 20)], [("zf", 0, 20)])
+    vcopy(T.mm[:], T.mli[:], [("mli", 0, 20)], [("mm", 0, 20)])
+    for f in prepare():
+        f()
+    unit(0)
+    quant("uq", "uqs", "ut", 0, 128)
+    do("v", lambda q: q.tensor_copy(T.u2[:, 0:128].bitcast(dt.uint32), T.uq[:, 0:128].bitcast(dt.uint32).indirect(T.ul[:, 0:8])),
+       [("uq", 0, 128), ("ul", 0, 8)], [("u2", 0, 128)])
+    scopy(T.u2s[:, 0:128], T.uqs[:, 0:128].indirect(T.ul[:, 0:8]), [("uqs", 0, 128), ("ul", 0, 8)], [("u2s", 0, 128)])
+    state_quant("x0", LO)
+    scores(LO)
+    state_quant("x0", UP)
+    scores(UP)
+    scores_low_out()
+    unit(1)
+    planes = [(b, half) for b in range(4) for half in (UP, LO)]
+    for b, half in planes[:3]:
+        plane("x0", b, half)
+
+    for r in range(3):
+        last = r == 2
+        x, xn = "x%d" % r, "x%d" % (r + 1)
+        nl, npl = "nl%d" % r, "np%d" % r
+        ql, qls, pl, pls = "ql%d" % r, "qls%d" % r, "pl%d" % r, "pls%d" % r
+        partner = T.cores[rank ^ STEP[r]]
+        engines = topo.engines(core, partner)[:8]
+        if r: arrival([(npl, 0, 20)], "arrl%d" % r, len(engines))
+        arrival([(pl, 0, H), (pls, 0, H)], "arrc%d" % r, 2 * len(engines))
+
+        hi, lo = (H, 0) if r else (0, H)
+        mates = "zo" if r else "mm"
+        for k, o in ((hi, op.is_gt), (lo, op.is_le)):
+            tt(cols("sw", k, k + H), psum(4, H), T.slo[:], o, [("bank4", 0, 512), ("slo", 0, H)], [("sw", k, k + H)])
+        pick("s", cols("gs", H, C), ("gs", H, C), "sw", C, mates, 10)
+        pick("s", cols("gs", 0, H), ("gs", 0, H), "sw", C, mates, 0)
+        if r == 0:
+            for b, half in planes[3:]:
+                plane("x0", b, half)
+            do("s", lambda q: q.activation(cols("aown", 0, LOW), cols("ident", 0, LOW), ActivationFunctionType.Identity, bias=float(WIN)), [("ident", 0, LOW)], [("aown", 0, LOW)])
+            for w in ("wa", "wb"):
+                scopy(cols(w, H, WIN), cols("ident", H, WIN), [("ident", H, WIN)], [(w, H, WIN)])
+                scopy(cols(w, WIN, CODES), cols("aown", 0, H), [("aown", 0, H)], [(w, WIN, CODES)])
+        scan_bits(0, "sw", hi)
+        choose("sc", 15, 16)
+        scan_bits(2 * H, "gs", H)
+        blend("kb")
+        scan_bits(H, "gs", 0)
+        if r == 0:
+            vcopy(T.bits[:], T.sc[:, 15:3 * H:16], [("sc", 0, 3 * H)], [("bits", 0, 30)])
+            send(partner, engines, [(T.bits[:], T.bitp[:], ("bits", 0, 30))], "arrl0")
+        turn("sc", 15, 16, nl)
+        if r: send(partner, engines, [(T[nl][:], T[npl][:], (nl, 0, 20))], "arrl%d" % r)
+
+        def total(half, b):
+            xp = "xp%d" % b
+            o = 10 if half == LO else 0
+            tt(T.z[:, 4 * half[0] + b:4 * half[1]:4], T[xp][:, 0:WIN].indirect(T[nl][:, o:o + 10]), T[x][:, 4 * half[0] + b:4 * half[1]:4], op.add,
+               [(xp, 0, WIN), (nl, o, o + 10), (x, half[0], half[1], b)], [("z", half[0], half[1], b)])
+
+        def layer(k, half):
+            for b in range(4):
+                product(k + b, "wq", "wqs", 128 * b, "qz", "qzs", half[0], H)
+
+        def made(q, b, k, half):
+            evacuate(q, T.a[:, 4 * half[0] + b:4 * half[1]:4], ("a", half[0], half[1], b), k + b, 0.015625)
+
+        for b in range(4):
+            total(LO, b)
+        total(UP, 0)
+        quant("qz", "qzs", "z", H, H, H)
+        layer(0, LO)
+        for b in range(4):
+            made("s", b, 0, LO)
+        for b in range(1, 4):
+            total(UP, b)
+        quant("qz", "qzs", "z", 0, H)
+        layer(4, UP)
+
+        def low_codes():
+            quant(ql, qls, "a", H, H)
+            send(partner, engines, [(T[ql][:, 0:H].bitcast(dt.uint8), T[pl][:, 0:H].bitcast(dt.uint8), (ql, 0, H)),
+                                    (T[qls][:, 0:H], T[pls][:, 0:H], (qls, 0, H))], "arrc%d" % r)
+
+        if r == 0:
+            vcopy(T.pzf[:], T.mlp[:], [("mlp", 0, 20)], [("pzf", 0, 20)])
+            quant("vq", "vqs", "vt", 0, 128)
+            steps = prepare("pzf", "pkb")
+            steps[0]()
+            low_codes()
+            steps[1]()
+            steps[2]()
+            choose("bitp", 0, 1)
+            blend("pkb")
+            turn("bitp", 0, 1, npl)
+
+        pick2("aown", LOW, "ident", WIN, npl, 0)
+        if r == 0:
+            unit(2)
+            unit(3)
+        else: low_codes()
+        pick2("wa", 0, "aown", WIN, nl, 10)
+        pick("s", T.su[:], ("su", 0, H), "aown", WIN, nl, 0)
+
+        def unpack(k, q, qs):
+            for b in range(4):
+                product(k + b, "eq", "eqs", 128 * b, q, qs, 0, H)
+
+        def unpacked(q, b, k, to):
+            evacuate(q, cols("b%d" % b, to, to + H), ("b%d" % b, to, to + H), k + b)
+
+        def beside(k):
+            if k < 4: made("v", k, 4, UP)
+            elif k == 4:
+                quant("qu", "qus", "a", 0, H)
+                unpack(0, "qu", "qus")
+            else: unpacked("v", k - 5, 0, H)
+
+        win, nxt = "wa", "wb"
+        for k in range(9):
+            if k < 8:
+                scn, lu = "scn%d" % (k % 3), "lu%d" % (k % 3)
+                scan(T[scn][:], (scn, 0, H), win, 0, H)
+                beside(k)
+                entries(T[lu][:], (lu, 0, 10), scn, 0, H, "bias")
+            pick("s", cols(nxt, 0, H), (nxt, 0, H), win, CODES, "lu%d" % (max(k - 1, 0) % 3), 0)
+            win, nxt = nxt, win
+        unpacked("s", 3, 0, H)
+        scan(T.ssu[:], ("ssu", 0, H), "su", 0, H)
+        entries(T.stu[:], ("stu", 0, 10), "ssu", 0, H, "bias")
+        unpack(4, pl, pls)
+        pick2("cf", H, win, CODES, npl, 10)
+        unpacked("s", 0, 4, 0)
+        unpacked("v", 2, 4, 0)
+        scan(cols("csc", H, C), ("csc", H, C), "cf", H, H)
+        unpacked("s", 1, 4, 0)
+        unpacked("v", 3, 4, 0)
+        entries(cols("zo", 10, 20), ("zo", 10, 20), "csc", H, H, "bz")
+        pick("s", cols("cf", 0, H), ("cf", 0, H), win, CODES, "stu", 0)
+
+        def renew(half, b):
+            a, e = address(half)
+            o = 10 if half == LO else 0
+            xp, bb = "xp%d" % b, "b%d" % b
+            tt(T[xn][:, 4 * half[0] + b:4 * half[1]:4], T[bb][:, 0:C].indirect(T.zo[:, o:o + 10]), cols(xp, a, e), op.add,
+               [(bb, 0, C), ("zo", o, o + 10), (xp, a, e)], [(xn, half[0], half[1], b)])
+
+        for b in range(4):
+            renew(LO, b)
+            if b == 1: scan(cols("csc", 0, H), ("csc", 0, H), "cf", 0, H)
+        entries(cols("zo", 0, 10), ("zo", 0, 10), "csc", 0, H, "bz")
+        steps = prepare()
+        if not last:
+            ts(T.zf[:], T.csc[:, 15:C:16], T.bz[:, 0:1], None, op.add, None, [("csc", 0, C), ("bz", 0, 1)], [("zf", 0, 20)])
+        state_quant(xn, LO)
+        if not last:
+            steps[0]()
+            scores(LO)
+            for b in range(4):
+                plane(xn, b, LO)
+        else:
+            product(0, "vq", "vqs", 0, "qx", "qxs", H, H)
+            scopy(cols("fin", 0, H), cols("ident", H, C), [("ident", H, C)], [("fin", 0, H)])
+            scopy(cols("fin", H, C), cols("ident", 0, H), [("ident", 0, H)], [("fin", H, C)])
+            pick("s", cols("mof", H, C), ("mof", H, C), "fin", C, "zo", 10)
+            pick("s", cols("mof", 0, H), ("mof", 0, H), "fin", C, "zo", 0)
+        for b in range(4):
+            renew(UP, b)
+            if b == 1 and not last: steps[1]()
+        if not last: steps[2]()
+        state_quant(xn, UP)
+        if not last:
+            scores(UP)
+            plane(xn, 0, UP)
+            plane(xn, 1, UP)
+            scores_low_out()
+            plane(xn, 2, UP)
+            plane(xn, 3, UP)
+        else:
+            product(4, "vq", "vqs", 0, "qx", "qxs", 0, H)
+
+    def store(q, out, in_, region):
+        do(q, lambda e: e.dma_start(out, in_), [region], [], "outs")
+
+    store("y", T.oc[:, 4 * H:4 * C], cols("qx", H, C).bitcast(dt.uint8), ("qx", H, C))
+    store("y", T.mo[:], T.mof[0:128:16, :], ("mof", 0, C))
+    evacuate("s", cols("yb", H, C), ("yb", H, C), 0)
+    store("s", T.y[:, H:C], cols("yb", H, C), ("yb", H, C))
+    store("y", T.oc[:, 0:4 * H], cols("qx", 0, H).bitcast(dt.uint8), ("qx", 0, H))
+    for k in range(4):
+        store("y", T.osc[4 * k:4 * k + 4, :], T.qxs[32 * k:32 * k + 4, 0:C], ("qxs", 0, C))
+    evacuate("s", cols("yb", 0, H), ("yb", 0, H), 4)
+    store("s", T.y[:, 0:H], cols("yb", 0, H), ("yb", 0, H))
+    for s in SEMAPHORES:
+        if count.get(s, 0): g.wait_ge(T.sem[s], count[s])

@@ -3,9 +3,10 @@ from concourse.mybir import dt, AluOpType, ActivationFunctionType
 BF, F32, I32, U16, U8, MX = "bfloat16", "float32", "int32", "uint16", "uint8", "float8_e4m3fn_x4"
 STEP = [1, 2, 4]
 C, H = 320, 160
-LOW = 256
-WIN = LOW + H
-CODES = WIN + H
+TOP = 2048
+WIN = TOP + H
+OWN, FAR = (162, 2), (488, 8)
+CODES = FAR[0] + FAR[1] * H
 
 SCRATCH = {
     "x0": ("sbuf", [128, 4 * C], BF), "x1": ("sbuf", [128, 4 * C], BF), "x2": ("sbuf", [128, 4 * C], BF), "x3": ("sbuf", [128, 4 * C], BF),
@@ -19,27 +20,26 @@ SCRATCH = {
     "qz": ("sbuf", [128, C], MX), "qzs": ("sbuf", [128, C], U8),
     "qu": ("sbuf", [128, H], MX), "qus": ("sbuf", [128, H], U8),
     "ps": ("psum", [128, 4096], F32),
-    "slo": ("sbuf", [128, H], F32), "sw": ("sbuf", [128, C], BF), "gs": ("sbuf", [128, C], BF), "sc": ("sbuf", [128, H + C], BF),
-    "mli": ("sbuf", [128, 20], I32), "zf": ("sbuf", [128, 20], F32), "wk": ("sbuf", [128, 20], F32), "kf": ("sbuf", [128, 20], F32),
+    "slo": ("sbuf", [128, H], F32), "sw": ("sbuf", [128, CODES], BF), "gs": ("sbuf", [128, C], BF), "sc": ("sbuf", [128, H + C], BF),
+    "mli": ("sbuf", [128, 20], I32), "wk": ("sbuf", [128, 20], F32), "kf": ("sbuf", [128, 20], F32),
     "kb": ("sbuf", [128, 20], F32), "mm": ("sbuf", [128, 20], U16), "cc": ("sbuf", [128, 30], F32), "kc": ("sbuf", [128, 40], F32),
-    "pq": ("sbuf", [128, 40], F32), "nf": ("sbuf", [128, 20], F32),
-    "mlp": ("sbuf", [128, 20], I32), "pzf": ("sbuf", [128, 20], F32), "pkb": ("sbuf", [128, 20], F32),
-    "bits": ("sbuf", [128, 30], F32), "bitp": ("sbuf", [128, 30], F32),
-    "ident": ("sbuf", [128, WIN], F32), "aown": ("sbuf", [128, WIN], F32), "wa": ("sbuf", [128, CODES], F32), "wb": ("sbuf", [128, CODES], F32),
-    "su": ("sbuf", [128, H], F32), "ssu": ("sbuf", [128, H], F32), "stu": ("sbuf", [128, 10], U16),
-    "cf": ("sbuf", [128, C], F32), "csc": ("sbuf", [128, C], F32), "zo": ("sbuf", [128, 20], U16),
-    "fin": ("sbuf", [128, C], F32), "mof": ("sbuf", [128, C], F32), "yb": ("sbuf", [128, C], F32),
-    "d0": ("sbuf", [128, C], F32), "ds": ("sbuf", [128, 16], F32), "d1": ("sbuf", [128, 16], F32), "d2": ("sbuf", [128, 16], F32), "tcol": ("sbuf", [128, 16], F32),
+    "pq": ("sbuf", [128, 40], F32), "nf": ("sbuf", [128, 20], F32), "ka": ("sbuf", [128, 60], F32),
+    "mlp": ("sbuf", [128, 20], I32), "pkb": ("sbuf", [128, 40], F32), "msg": ("sbuf", [128, 40], BF), "msp": ("sbuf", [128, 40], BF),
+    "ident": ("sbuf", [128, H], BF), "tab": ("sbuf", [128, WIN], BF), "gw": ("sbuf", [128, WIN], BF),
+    "wa": ("sbuf", [128, WIN], BF), "wb": ("sbuf", [128, WIN], BF),
+    "su": ("sbuf", [128, H], BF), "ssu": ("sbuf", [128, H], BF), "stu": ("sbuf", [128, 10], U16),
+    "cf": ("sbuf", [128, C], BF), "csc": ("sbuf", [128, C], BF), "zo": ("sbuf", [128, 20], U16),
+    "fin": ("sbuf", [128, CODES], F32), "mof": ("sbuf", [128, C], F32), "yb": ("sbuf", [128, C], F32),
+    "d0": ("sbuf", [128, C], BF), "ds": ("sbuf", [128, 16], F32), "d1": ("sbuf", [128, 16], F32), "d2": ("sbuf", [128, 16], F32), "tcol": ("sbuf", [128, 16], F32),
     "pix": ("sbuf", [128, 20], I32), "qi": ("sbuf", [128, 20], I32), "qo": ("sbuf", [128, 20], U16), "qf": ("sbuf", [128, 1], F32), "q1": ("sbuf", [128, 1], F32),
-    "e0": ("sbuf", [128, H], BF), "es": ("sbuf", [128, 16], F32), "e1": ("sbuf", [128, 16], F32), "e2": ("sbuf", [128, 16], F32),
-    "bias": ("sbuf", [128, 1], F32), "bb": ("sbuf", [128, 1], F32), "bm": ("sbuf", [128, 1], F32), "bz": ("sbuf", [128, 1], F32),
+    "e0": ("sbuf", [128, H], BF), "es": ("sbuf", [128, 16], F32), "col": ("sbuf", [128, 8], F32),
     "uli": ("sbuf", [128, 8], I32), "ul": ("sbuf", [128, 8], U16),
 }
 for _b in range(4):
     SCRATCH["xp%d" % _b] = ("sbuf", [128, WIN], BF)
-    SCRATCH["b%d" % _b] = ("sbuf", [128, C], F32)
+    SCRATCH["b%d" % _b] = ("sbuf", [128, CODES], BF)
 for _r in range(3):
-    SCRATCH["scn%d" % _r] = ("sbuf", [128, H], F32)
+    SCRATCH["scn%d" % _r] = ("sbuf", [128, H], BF)
     SCRATCH["lu%d" % _r] = ("sbuf", [128, 10], U16)
     SCRATCH["nl%d" % _r] = ("sbuf", [128, 20], U16)
     SCRATCH["np%d" % _r] = ("sbuf", [128, 20], U16)
@@ -52,6 +52,7 @@ for _r in range(3):
     SEMAPHORES += ["arrl%d" % _r, "arrc%d" % _r]
 
 LO, UP = (H, C), (0, H)
+BB, BM, INV, S_OWN, S_CUT, S_FAR, B_OWN, B_FAR = range(8)
 
 
 def rank_program(g, core, T, topo):
@@ -125,10 +126,17 @@ def rank_program(g, core, T, topo):
         record("remote", [], [full(r) for r in regions], sem, n)
 
     op = AluOpType
-    COPY = ActivationFunctionType.Copy
+    COPY, SAME = ActivationFunctionType.Copy, ActivationFunctionType.Identity
 
     def cols(name, a, b):
         return T[name][:, a:b]
+
+    def col(k):
+        return T.col[:, k:k + 1]
+
+    def spots(name, code):
+        a, e = code[0] - 1, code[0] - 1 + code[1] * H
+        return T[name][:, a:e:code[1]], (name, a, e)
 
     def tt(out, in0, in1, o, reads, writes):
         do("v", lambda q: q.tensor_tensor(out, in0, in1, o), reads, writes)
@@ -146,23 +154,21 @@ def rank_program(g, core, T, topo):
         if scale == 1.0: do("s", lambda q: q.activation(out, in_, COPY), reads, writes)
         else: do("s", lambda q: q.activation(out, in_, COPY, scale=scale), reads, writes)
 
-    def pick(q, out, oreg, win, wn, off, a):
+    def line(out, in_, scale, bias, reads, writes):
+        do("s", lambda q: q.activation(out, in_, SAME, bias=bias, scale=scale), reads, writes)
+
+    def pick(q, name, o, win, wn, off, a, n=10):
         f = vcopy if q == "v" else scopy
-        f(out, T[win][:, 0:wn].indirect(T[off][:, a:a + 10]), [(win, 0, wn), (off, a, a + 10)], [oreg])
+        f(cols(name, o, o + 16 * n), T[win][:, 0:wn].indirect(T[off][:, a:a + n]), [(win, 0, wn), (off, a, a + n)], [(name, o, o + 16 * n)])
 
-    def scan(out, oreg, src, a, n):
-        do("v", lambda q: q.tensor_tensor_scan(out, T.d0[:, 0:n], T[src][:, a:a + n], 0.0, op.add, op.min), [("d0", 0, C), (src, a, a + n)], [oreg])
+    def scan(out, src, n):
+        do("v", lambda q: q.tensor_tensor_scan(cols(out, 0, n), cols("d0", 0, n), cols(src, 0, n), 0.0, op.mult, op.max), [("d0", 0, C), (src, 0, n)], [(out, 0, n)])
 
-    def scan_bits(a, src, b):
-        do("v", lambda q: q.tensor_tensor_scan(cols("sc", a, a + H), T.e0[:], T[src][:, b:b + H], 0.0, op.add, op.min), [("e0", 0, H), (src, b, b + H)], [("sc", a, a + H)])
+    def scan_bits(a, src, region):
+        do("v", lambda q: q.tensor_tensor_scan(cols("sc", a, a + H), T.e0[:], src, 0.0, op.add, op.min), [("e0", 0, H), region], [("sc", a, a + H)])
 
-    def pick2(name, o, win, wn, off, a):
-        for q, c, d in (("v", 0, 6), ("s", 6, 10)):
-            f = vcopy if q == "v" else scopy
-            f(cols(name, o + 16 * c, o + 16 * d), T[win][:, 0:wn].indirect(T[off][:, a + c:a + d]), [(win, 0, wn), (off, a + c, a + d)], [(name, o + 16 * c, o + 16 * d)])
-
-    def entries(out, oreg, src, a, n, col):
-        ts(out, T[src][:, a + 15:a + n:16], T[col][:, 0:1], None, op.add, None, [(src, a, a + n), (col, 0, 1)], [oreg])
+    def entries(out, src, n):
+        ts(cols(out, 0, n // 16), T[src][:, 15:n:16], col(INV), -1.0, op.mult, op.add, [(src, 0, n), ("col", INV, INV + 1)], [(out, 0, n // 16)])
 
     def quant(out, scales, tile, a, n, dst=0):
         do("v", lambda q: q.quantize_mx(T[out][:, dst:dst + n], T[scales][:, dst:dst + n], T[tile][:, 4 * a:4 * (a + n)]),
@@ -182,44 +188,53 @@ def rank_program(g, core, T, topo):
     def load(q, out, in_, region, sem):
         do(q, lambda e: e.dma_start(out, in_), [], [region], sem)
 
-    load("y", cols("x0", 4 * H, 4 * C), T.x[:, 4 * H:4 * C], ("x0", H, C), "ldxl")
     load("s", T.mli[:], T.ml[:], ("mli", 0, 20), "ldm")
-    load("y", cols("x0", 0, 4 * H), T.x[:, 0:4 * H], ("x0", 0, H), "ldxu")
     load("s", T.ut[:], T.u[:], ("ut", 0, 128), "ldu")
+    load("y", cols("x0", 4 * H, 4 * C), T.x[:, 4 * H:4 * C], ("x0", H, C), "ldxl")
+    load("y", cols("x0", 0, 4 * H), T.x[:, 0:4 * H], ("x0", 0, H), "ldxu")
     load("y", T.wq[:].bitcast(dt.uint8), T.wc[:], ("wq", 0, 512), "ldw")
-    load("s", T.wqs[:], T.ws[:], ("wqs", 0, 512), "ldws")
+    load("y", T.wqs[:], T.ws[:], ("wqs", 0, 512), "ldws")
     load("y", T.vt[:], T.v[:], ("vt", 0, 128), "ldv")
 
     do("v", lambda q: q.memset(T.eo[:], 1.0), [], [("eo", 0, 528)])
     do("g", lambda q: q.iota(T.pix[:], [[0, 20]], 0, 1), [], [("pix", 0, 20)])
     do("g", lambda q: q.iota(T.tcol[:], [[1, 16]], 0, 0, allow_small_or_imprecise_dtypes=True), [], [("tcol", 0, 16)])
-    do("g", lambda q: q.affine_select(T.et[:], T.eo[:], [[-1, 528]], op.is_equal, 0.0, 3, 4), [("eo", 0, 528)], [("et", 0, 528)])
     do("g", lambda q: q.iota(T.uli[:], [[16, 8]], 0, 0), [], [("uli", 0, 8)])
-    do("g", lambda q: q.iota(T.ident[:], [[1, WIN]], 0, 0, allow_small_or_imprecise_dtypes=True), [], [("ident", 0, WIN)])
+    do("g", lambda q: q.iota(T.ident[:], [[1, H]], 0, 0, allow_small_or_imprecise_dtypes=True), [], [("ident", 0, H)])
+    do("g", lambda q: q.affine_select(T.et[:], T.eo[:], [[-1, 528]], op.is_equal, 0.0, 3, 4), [("eo", 0, 528)], [("et", 0, 528)])
     first = T.cores[rank ^ STEP[0]]
-    lanes = topo.engines(core, first)[:8]
+    lanes = topo.engines(core, first)
     arrival([("mlp", 0, 20)], "arrm", len(lanes))
-    arrival([("bitp", 0, 30)], "arrl0", len(lanes))
+    arrival([("msp", 0, 40)], "arrl0", len(lanes))
     send(first, lanes, [(T.mli[:], T.mlp[:], ("mli", 0, 20))], "arrm")
     do("v", lambda q: q.tensor_scalar(T.qi[:], T.pix[:], 15, None, op.bitwise_and), [("pix", 0, 20)], [("qi", 0, 20)])
+    vcopy(T.ul[:], T.uli[:], [("uli", 0, 8)], [("ul", 0, 8)])
     vcopy(T.qf[:], cols("qi", 0, 1), [("qi", 0, 1)], [("qf", 0, 1)])
     vcopy(T.qo[:], T.qi[:], [("qi", 0, 20)], [("qo", 0, 20)])
     ts(T.q1[:], T.qf[:], 1.0, None, op.add, None, [("qf", 0, 1)], [("q1", 0, 1)])
-    ts(T.d2[:], T.tcol[:], T.qf[:, 0:1], 4096.0, op.is_equal, op.mult, [("tcol", 0, 16), ("qf", 0, 1)], [("d2", 0, 16)])
-    ts(T.d1[:], T.tcol[:], T.q1[:, 0:1], -1024.0, op.is_equal, op.mult, [("tcol", 0, 16), ("q1", 0, 1)], [("d1", 0, 16)])
+    ts(T.d2[:], T.tcol[:], T.qf[:, 0:1], -1.0, op.is_equal, op.mult, [("tcol", 0, 16), ("qf", 0, 1)], [("d2", 0, 16)])
+    ts(col(BB), T.qf[:], 14.5, 2.0, op.is_lt, op.mult, [("qf", 0, 1)], [("col", BB, BB + 1)])
+    ts(T.d1[:], T.tcol[:], T.q1[:, 0:1], TOP - 1.0, op.is_equal, op.mult, [("tcol", 0, 16), ("q1", 0, 1)], [("d1", 0, 16)])
+    ts(col(INV), T.qf[:], 14.5, 1.0 / TOP, op.is_gt, op.max, [("qf", 0, 1)], [("col", INV, INV + 1)])
     tt(T.ds[:], T.d2[:], T.d1[:], op.add, [("d2", 0, 16), ("d1", 0, 16)], [("ds", 0, 16)])
-    scopy(T.d0[:], T.ds[:].indirect(T.qo[:, 0:20]), [("ds", 0, 16), ("qo", 0, 20)], [("d0", 0, C)])
-    ts(T.bias[:], T.qf[:], 14.5, 1024.0, op.is_lt, op.mult, [("qf", 0, 1)], [("bias", 0, 1)])
-    ts(T.e2[:], T.tcol[:], T.qf[:, 0:1], 8.0, op.is_equal, op.mult, [("tcol", 0, 16), ("qf", 0, 1)], [("e2", 0, 16)])
-    ts(T.e1[:], T.tcol[:], T.q1[:, 0:1], -2.0, op.is_equal, op.mult, [("tcol", 0, 16), ("q1", 0, 1)], [("e1", 0, 16)])
-    ts(T.bb[:], T.qf[:], 14.5, 2.0, op.is_lt, op.mult, [("qf", 0, 1)], [("bb", 0, 1)])
-    tt(T.es[:], T.e2[:], T.e1[:], op.add, [("e2", 0, 16), ("e1", 0, 16)], [("es", 0, 16)])
+    ts(col(BM), col(BB), -1.0, None, op.add, None, [("col", BB, BB + 1)], [("col", BM, BM + 1)])
+    ts(T.es[:], T.ds[:], 0.25, -8.0, op.min, op.mult, [("ds", 0, 16)], [("es", 0, 16)])
+    line(T.d0[:], T.ds[:].indirect(T.qo[:, 0:20]), 1.0, 1.0, [("ds", 0, 16), ("qo", 0, 20)], [("d0", 0, C)])
     scopy(T.e0[:], T.es[:].indirect(T.qo[:, 0:10]), [("es", 0, 16), ("qo", 0, 10)], [("e0", 0, H)])
-    ts(T.bm[:], T.bb[:], -1.0, None, op.add, None, [("bb", 0, 1)], [("bm", 0, 1)])
-    ts(T.bz[:], T.bias[:], -float(LOW), None, op.add, None, [("bias", 0, 1)], [("bz", 0, 1)])
-    vcopy(T.ul[:], T.uli[:], [("uli", 0, 8)], [("ul", 0, 8)])
-    for b in range(4):
-        do("v", lambda q: q.memset(cols("xp%d" % b, H, LOW), 0.0), [], [("xp%d" % b, H, LOW)])
+    for k, src, scale, bias in ((S_OWN, INV, 1.0 / (OWN[1] * TOP), 0.0), (S_CUT, INV, -2.0, 0.0), (S_FAR, INV, 1.0 / (FAR[1] * TOP), 0.0),
+                                (B_OWN, BB, 1.0, -OWN[0] / (OWN[1] * TOP)), (B_FAR, BB, 1.0, -FAR[0] / (FAR[1] * TOP))):
+        line(col(k), col(src), scale, bias, [("col", src, src + 1)], [("col", k, k + 1)])
+
+    def table(out, region, code):
+        ts(out, T.ident[:], float(code[1]), float(code[0]), op.mult, op.add, [("ident", 0, H)], [region])
+
+    table(cols("tab", 0, H), ("tab", 0, H), (1, 1))
+    table(cols("gw", 0, H), ("gw", 0, H), FAR)
+    for w in ("tab", "wb"):
+        table(cols(w, TOP, WIN), (w, TOP, WIN), OWN)
+    for w in ("wa", "wb"):
+        for code in (OWN, FAR):
+            table(*spots(w, code), code)
 
     def unit(b):
         do("v", lambda q: q.quantize_mx(cols("eq", 128 * b, 128 * b + 128), cols("eqs", 128 * b, 128 * b + 128), cols("et", 3 - b, 515 - b)),
@@ -232,7 +247,7 @@ def rank_program(g, core, T, topo):
         quant("qx", "qxs", x, half[0], H, half[0])
 
     def address(half):
-        return (LOW, WIN) if half == LO else (0, H)
+        return (0, H) if half == LO else (TOP, WIN)
 
     def plane(x, b, half):
         a, e = address(half)
@@ -241,44 +256,48 @@ def rank_program(g, core, T, topo):
     def scores_low_out():
         evacuate("s", T.slo[:], ("slo", 0, H), 0)
 
-    def prepare(zf="zf", kb="kb"):
-        return [lambda: ts(T.wk[:], T[zf][:], H - 0.5, -float(H), op.is_gt, op.mult, [(zf, 0, 20)], [("wk", 0, 20)]),
-                lambda: tt(T.kf[:], T[zf][:], T.wk[:], op.add, [(zf, 0, 20), ("wk", 0, 20)], [("kf", 0, 20)]),
-                lambda: ts(T[kb][:], T.kf[:], 1.0 / LOW, T.bb[:, 0:1], op.mult, op.add, [("kf", 0, 20), ("bb", 0, 1)], [(kb, 0, 20)])]
+    def places(m, outs):
+        return [lambda: ts(T.wk[:], T[m][:], H - 0.5, -float(H), op.is_gt, op.mult, [(m, 0, 20)], [("wk", 0, 20)]),
+                lambda: tt(T.kf[:], T[m][:], T.wk[:], op.add, [(m, 0, 20), ("wk", 0, 20)], [("kf", 0, 20)]),
+                lambda: [ts(out, T.kf[:], 1.0 / TOP, col(BB), op.mult, op.add, [("kf", 0, 20), ("col", BB, BB + 1)], [region]) for out, region in outs]]
 
-    def choose(bits, a, step):
-        for k, col, f in ((10, "bm", 4.0), (20, "bb", -4.0), (0, "bb", -4.0)):
-            ts(cols("cc", k, k + 10), T[bits][:, a:10 * step:step], T[col][:, 0:1], f, op.add, op.mult,
-               [(bits, 0, 10 * step), (col, 0, 1)], [("cc", k, k + 10)])
+    def choose():
+        for k, c, f in ((10, BM, 4.0), (20, BB, -4.0), (0, BB, -4.0)):
+            ts(cols("cc", k, k + 10), T.sc[:, 15:H:16], col(c), f, op.add, op.mult, [("sc", 0, H), ("col", c, c + 1)], [("cc", k, k + 10)])
 
-    def blend(kb):
+    def blend():
         for k in (10, 0):
-            tt(cols("kc", 2 * k, 2 * k + 20), cols("cc", k, k + 20), T[kb][:], op.add, [("cc", k, k + 20), (kb, 0, 20)], [("kc", 2 * k, 2 * k + 20)])
+            tt(cols("kc", 2 * k, 2 * k + 20), cols("cc", k, k + 20), T.kb[:], op.add, [("cc", k, k + 20), ("kb", 0, 20)], [("kc", 2 * k, 2 * k + 20)])
 
-    def turn(bits, a, step, out):
-        n = 10 * step
-        for k in (20, 0):
-            tt(cols("pq", k, k + 20), T[bits][:, n + a:3 * n:step], cols("kc", k, k + 20), op.add, [(bits, n, 3 * n), ("kc", k, k + 20)], [("pq", k, k + 20)])
-        for k in (20, 0):
-            tt(cols("nf", k // 2, k // 2 + 10), cols("pq", k, k + 10), cols("pq", k + 10, k + 20), op.max, [("pq", k, k + 20)], [("nf", k // 2, k // 2 + 10)])
-        for k in (10, 0):
-            ts(cols(out, k, k + 10), cols("nf", k, k + 10), float(LOW), None, op.mult, None, [("nf", k, k + 10)], [(out, k, k + 10)])
+    def offers(out, add, a):
+        for w in (1, 0):
+            tt(T[out][:, w:40:2], T.sc[:, H + 15:3 * H:16], cols(add, a * w, a * w + 20), op.add, [("sc", H, 3 * H), (add, a * w, a * w + 20)], [(out, 0, 40, w)])
 
-    vcopy(T.zf[:], T.mli[:], [("mli", 0, 20)], [("zf", 0, 20)])
+    def larger():
+        tt(T.nf[:], cols("pq", 0, 20), cols("pq", 20, 40), op.max, [("pq", 0, 40)], [("nf", 0, 20)])
+
+    def addresses(out):
+        for w in (1, 0):
+            ts(cols(out, 10 * w, 10 * w + 10), T.nf[:, w:20:2], float(TOP), None, op.mult, None, [("nf", 0, 20)], [(out, 10 * w, 10 * w + 10)])
+
+    steps = places("mli", [(T.kb[:], ("kb", 0, 20))])
+    steps[0]()
     vcopy(T.mm[:], T.mli[:], [("mli", 0, 20)], [("mm", 0, 20)])
-    for f in prepare():
-        f()
     unit(0)
+    steps[1]()
+    unit(1)
+    steps[2]()
     quant("uq", "uqs", "ut", 0, 128)
+    state_quant("x0", LO)
     do("v", lambda q: q.tensor_copy(T.u2[:, 0:128].bitcast(dt.uint32), T.uq[:, 0:128].bitcast(dt.uint32).indirect(T.ul[:, 0:8])),
        [("uq", 0, 128), ("ul", 0, 8)], [("u2", 0, 128)])
     scopy(T.u2s[:, 0:128], T.uqs[:, 0:128].indirect(T.ul[:, 0:8]), [("uqs", 0, 128), ("ul", 0, 8)], [("u2s", 0, 128)])
-    state_quant("x0", LO)
     scores(LO)
     state_quant("x0", UP)
     scores(UP)
     scores_low_out()
-    unit(1)
+    unit(2)
+    unit(3)
     planes = [(b, half) for b in range(4) for half in (UP, LO)]
     for b, half in planes[:3]:
         plane("x0", b, half)
@@ -289,39 +308,40 @@ def rank_program(g, core, T, topo):
         nl, npl = "nl%d" % r, "np%d" % r
         ql, qls, pl, pls = "ql%d" % r, "qls%d" % r, "pl%d" % r, "pls%d" % r
         partner = T.cores[rank ^ STEP[r]]
-        engines = topo.engines(core, partner)[:8]
+        engines = topo.engines(core, partner)
         if r: arrival([(npl, 0, 20)], "arrl%d" % r, len(engines))
         arrival([(pl, 0, H), (pls, 0, H)], "arrc%d" % r, 2 * len(engines))
 
-        hi, lo = (H, 0) if r else (0, H)
+        upper, lower = (spots("sw", OWN), spots("sw", FAR)) if r else ((cols("sw", 0, H), ("sw", 0, H)), (cols("sw", H, C), ("sw", H, C)))
         mates = "zo" if r else "mm"
-        for k, o in ((hi, op.is_gt), (lo, op.is_le)):
-            tt(cols("sw", k, k + H), psum(4, H), T.slo[:], o, [("bank4", 0, 512), ("slo", 0, H)], [("sw", k, k + H)])
-        pick("s", cols("gs", H, C), ("gs", H, C), "sw", C, mates, 10)
-        pick("s", cols("gs", 0, H), ("gs", 0, H), "sw", C, mates, 0)
+        for (view, region), o in ((lower, op.is_gt), (upper, op.is_le)):
+            tt(view, psum(4, H), T.slo[:], o, [("bank4", 0, 512), ("slo", 0, H)], [region])
+        pick("s", "gs", H, "sw", CODES, mates, 10)
+        pick("s", "gs", 0, "sw", CODES, mates, 0)
         if r == 0:
             for b, half in planes[3:]:
                 plane("x0", b, half)
-            do("s", lambda q: q.activation(cols("aown", 0, LOW), cols("ident", 0, LOW), ActivationFunctionType.Identity, bias=float(WIN)), [("ident", 0, LOW)], [("aown", 0, LOW)])
-            for w in ("wa", "wb"):
-                scopy(cols(w, H, WIN), cols("ident", H, WIN), [("ident", H, WIN)], [(w, H, WIN)])
-                scopy(cols(w, WIN, CODES), cols("aown", 0, H), [("aown", 0, H)], [(w, WIN, CODES)])
-        scan_bits(0, "sw", hi)
-        choose("sc", 15, 16)
-        scan_bits(2 * H, "gs", H)
-        blend("kb")
-        scan_bits(H, "gs", 0)
+        scan_bits(0, *lower)
+        if r == 1: quant("vq", "vqs", "vt", 0, 128)
+        choose()
+        scan_bits(2 * H, cols("gs", H, C), ("gs", H, C))
+        blend()
+        scan_bits(H, cols("gs", 0, H), ("gs", 0, H))
         if r == 0:
-            vcopy(T.bits[:], T.sc[:, 15:3 * H:16], [("sc", 0, 3 * H)], [("bits", 0, 30)])
-            send(partner, engines, [(T.bits[:], T.bitp[:], ("bits", 0, 30))], "arrl0")
-        turn("sc", 15, 16, nl)
+            offers("msg", "cc", 10)
+            send(partner, engines, [(T.msg[:], T.msp[:], ("msg", 0, 40))], "arrl0")
+        offers("pq", "kc", 20)
+        larger()
+        addresses(nl)
         if r: send(partner, engines, [(T[nl][:], T[npl][:], (nl, 0, 20))], "arrl%d" % r)
+        pick("s", "gw", TOP, "tab", WIN, nl, 10)
 
-        def total(half, b):
+        def total(half, b, c=0, d=10):
             xp = "xp%d" % b
             o = 10 if half == LO else 0
-            tt(T.z[:, 4 * half[0] + b:4 * half[1]:4], T[xp][:, 0:WIN].indirect(T[nl][:, o:o + 10]), T[x][:, 4 * half[0] + b:4 * half[1]:4], op.add,
-               [(xp, 0, WIN), (nl, o, o + 10), (x, half[0], half[1], b)], [("z", half[0], half[1], b)])
+            lo, hi = half[0] + 16 * c, half[0] + 16 * d
+            tt(T.z[:, 4 * lo + b:4 * hi:4], T[xp][:, 0:WIN].indirect(T[nl][:, o + c:o + d]), T[x][:, 4 * lo + b:4 * hi:4], op.add,
+               [(xp, 0, WIN), (nl, o + c, o + d), (x, lo, hi, b)], [("z", lo, hi, b)])
 
         def layer(k, half):
             for b in range(4):
@@ -330,111 +350,99 @@ def rank_program(g, core, T, topo):
         def made(q, b, k, half):
             evacuate(q, T.a[:, 4 * half[0] + b:4 * half[1]:4], ("a", half[0], half[1], b), k + b, 0.015625)
 
-        for b in range(4):
-            total(LO, b)
-        total(UP, 0)
-        quant("qz", "qzs", "z", H, H, H)
-        layer(0, LO)
-        for b in range(4):
-            made("s", b, 0, LO)
-        for b in range(1, 4):
-            total(UP, b)
-        quant("qz", "qzs", "z", 0, H)
-        layer(4, UP)
-
         def low_codes():
             quant(ql, qls, "a", H, H)
             send(partner, engines, [(T[ql][:, 0:H].bitcast(dt.uint8), T[pl][:, 0:H].bitcast(dt.uint8), (ql, 0, H)),
                                     (T[qls][:, 0:H], T[pls][:, 0:H], (qls, 0, H))], "arrc%d" % r)
 
-        if r == 0:
-            vcopy(T.pzf[:], T.mlp[:], [("mlp", 0, 20)], [("pzf", 0, 20)])
-            quant("vq", "vqs", "vt", 0, 128)
-            steps = prepare("pzf", "pkb")
-            steps[0]()
-            low_codes()
-            steps[1]()
-            steps[2]()
-            choose("bitp", 0, 1)
-            blend("pkb")
-            turn("bitp", 0, 1, npl)
-
-        pick2("aown", LOW, "ident", WIN, npl, 0)
-        if r == 0:
-            unit(2)
-            unit(3)
-        else: low_codes()
-        pick2("wa", 0, "aown", WIN, nl, 10)
-        pick("s", T.su[:], ("su", 0, H), "aown", WIN, nl, 0)
-
         def unpack(k, q, qs):
             for b in range(4):
                 product(k + b, "eq", "eqs", 128 * b, q, qs, 0, H)
 
-        def unpacked(q, b, k, to):
-            evacuate(q, cols("b%d" % b, to, to + H), ("b%d" % b, to, to + H), k + b)
+        def unpacked(q, b, k, code):
+            evacuate(q, *spots("b%d" % b, code), k + b)
 
-        def beside(k):
-            if k < 4: made("v", k, 4, UP)
-            elif k == 4:
-                quant("qu", "qus", "a", 0, H)
-                unpack(0, "qu", "qus")
-            else: unpacked("v", k - 5, 0, H)
+        steps = places("mlp", [(T.pkb[:, w:40:2], ("pkb", 0, 40, w)) for w in range(2)])
+        for b in range(4):
+            total(LO, b)
+            if r == 0 and b < 3: steps[b]()
+        total(UP, 0, 0, 4)
+        quant("qz", "qzs", "z", H, H, H)
+        layer(0, LO)
+        if r == 0: tt(T.pq[:], T.msp[:], T.pkb[:], op.add, [("msp", 0, 40), ("pkb", 0, 40)], [("pq", 0, 40)])
+        total(UP, 0, 4, 10)
+        if r == 0: larger()
+        total(UP, 1, 0, 4)
+        if r == 0: addresses(npl)
+        total(UP, 1, 4, 10)
 
+        pick("s", "wa", 0, "gw", WIN, npl, 0)
+        pick("s", "su", 0, "gw", WIN, npl, 10)
+        made("s", 0, 0, LO)
+        made("s", 1, 0, LO)
+
+        def upper_layer():
+            quant("qz", "qzs", "z", 0, H)
+            layer(4, UP)
+
+        def upper_codes():
+            quant("qu", "qus", "a", 0, H)
+            unpack(0, "qu", "qus")
+            unpack(4, pl, pls)
+
+        behind_scan = {0: lambda: total(UP, 2, 0, 4), 1: lambda: total(UP, 3, 0, 4), 2: upper_layer, 3: lambda: entries("stu", "ssu", H),
+                       4: lambda: made("v", 1, 4, UP), 5: upper_codes, 7: lambda: unpacked("v", 1, 0, OWN)}
+        behind_list = {0: lambda: (made("v", 2, 0, LO), made("v", 3, 0, LO), total(UP, 2, 4, 10), low_codes()), 1: lambda: total(UP, 3, 4, 10),
+                       2: lambda: scan("ssu", "su", H), 3: lambda: made("v", 0, 4, UP), 4: lambda: made("v", 3, 4, UP), 6: lambda: unpacked("v", 0, 0, OWN),
+                       7: lambda: [unpacked("v", b, 0, OWN) for b in range(2, 4)]}
+        behind_pick = {4: lambda: made("s", 2, 4, UP)}
         win, nxt = "wa", "wb"
         for k in range(9):
             if k < 8:
                 scn, lu = "scn%d" % (k % 3), "lu%d" % (k % 3)
-                scan(T[scn][:], (scn, 0, H), win, 0, H)
-                beside(k)
-                entries(T[lu][:], (lu, 0, 10), scn, 0, H, "bias")
-            pick("s", cols(nxt, 0, H), (nxt, 0, H), win, CODES, "lu%d" % (max(k - 1, 0) % 3), 0)
+                scan(scn, win, H)
+                if k in behind_scan: behind_scan[k]()
+                entries(lu, scn, H)
+            if k == 4: behind_pick[k]()
+            if k in behind_list: behind_list[k]()
+            pick("s", nxt, 0, win, CODES, "lu%d" % (max(k - 1, 0) % 3), 0)
             win, nxt = nxt, win
-        unpacked("s", 3, 0, H)
-        scan(T.ssu[:], ("ssu", 0, H), "su", 0, H)
-        entries(T.stu[:], ("stu", 0, 10), "ssu", 0, H, "bias")
-        unpack(4, pl, pls)
-        pick2("cf", H, win, CODES, npl, 10)
-        unpacked("s", 0, 4, 0)
-        unpacked("v", 2, 4, 0)
-        scan(cols("csc", H, C), ("csc", H, C), "cf", H, H)
-        unpacked("s", 1, 4, 0)
-        unpacked("v", 3, 4, 0)
-        entries(cols("zo", 10, 20), ("zo", 10, 20), "csc", H, H, "bz")
-        pick("s", cols("cf", 0, H), ("cf", 0, H), win, CODES, "stu", 0)
+        pick("v", "cf", 0, win, WIN, nl, 0)
+        pick("s", "cf", H, win, CODES, "stu", 0)
+        for b in range(4):
+            unpacked("s", b, 4, FAR)
+        scan("csc", "cf", C)
+        entries("zo", "csc", C)
 
         def renew(half, b):
             a, e = address(half)
             o = 10 if half == LO else 0
             xp, bb = "xp%d" % b, "b%d" % b
-            tt(T[xn][:, 4 * half[0] + b:4 * half[1]:4], T[bb][:, 0:C].indirect(T.zo[:, o:o + 10]), cols(xp, a, e), op.add,
-               [(bb, 0, C), ("zo", o, o + 10), (xp, a, e)], [(xn, half[0], half[1], b)])
+            tt(T[xn][:, 4 * half[0] + b:4 * half[1]:4], T[bb][:, 0:CODES].indirect(T.zo[:, o:o + 10]), cols(xp, a, e), op.add,
+               [(bb, 0, CODES), ("zo", o, o + 10), (xp, a, e)], [(xn, half[0], half[1], b)])
 
+        if not last:
+            for k, (s, b) in enumerate(((S_OWN, col(B_OWN)), (S_CUT, 2.0 * (FAR[0] - 6)), (S_FAR, col(B_FAR)))):
+                line(cols("ka", 20 * k, 20 * k + 20), T.csc[:, 15:C:16], col(s), b, [("csc", 0, C), ("col", 0, 8)], [("ka", 20 * k, 20 * k + 20)])
+        else:
+            for code, first_column in ((OWN, 0.0), (FAR, float(H))):
+                view, region = spots("fin", code)
+                line(view, T.ident[:], 1.0, first_column, [("ident", 0, H)], [region])
+            pick("s", "mof", 0, "fin", CODES, "zo", 0, 20)
         for b in range(4):
             renew(LO, b)
-            if b == 1: scan(cols("csc", 0, H), ("csc", 0, H), "cf", 0, H)
-        entries(cols("zo", 0, 10), ("zo", 0, 10), "csc", 0, H, "bz")
-        steps = prepare()
-        if not last:
-            ts(T.zf[:], T.csc[:, 15:C:16], T.bz[:, 0:1], None, op.add, None, [("csc", 0, C), ("bz", 0, 1)], [("zf", 0, 20)])
+            if not last: plane(xn, b, LO)
+        renew(UP, 0)
         state_quant(xn, LO)
-        if not last:
-            steps[0]()
-            scores(LO)
-            for b in range(4):
-                plane(xn, b, LO)
-        else:
-            product(0, "vq", "vqs", 0, "qx", "qxs", H, H)
-            scopy(cols("fin", 0, H), cols("ident", H, C), [("ident", H, C)], [("fin", 0, H)])
-            scopy(cols("fin", H, C), cols("ident", 0, H), [("ident", 0, H)], [("fin", H, C)])
-            pick("s", cols("mof", H, C), ("mof", H, C), "fin", C, "zo", 10)
-            pick("s", cols("mof", 0, H), ("mof", 0, H), "fin", C, "zo", 0)
-        for b in range(4):
+        if not last: scores(LO)
+        else: product(0, "vq", "vqs", 0, "qx", "qxs", H, H)
+        for b in range(1, 4):
             renew(UP, b)
-            if b == 1 and not last: steps[1]()
-        if not last: steps[2]()
+        if not last:
+            tt(T.kf[:], cols("ka", 0, 20), cols("ka", 20, 40), op.min, [("ka", 0, 40)], [("kf", 0, 20)])
         state_quant(xn, UP)
         if not last:
+            tt(T.kb[:], T.kf[:], cols("ka", 40, 60), op.max, [("kf", 0, 20), ("ka", 40, 60)], [("kb", 0, 20)])
             scores(UP)
             plane(xn, 0, UP)
             plane(xn, 1, UP)
@@ -447,8 +455,8 @@ def rank_program(g, core, T, topo):
     def store(q, out, in_, region):
         do(q, lambda e: e.dma_start(out, in_), [region], [], "outs")
 
-    store("y", T.oc[:, 4 * H:4 * C], cols("qx", H, C).bitcast(dt.uint8), ("qx", H, C))
     store("y", T.mo[:], T.mof[0:128:16, :], ("mof", 0, C))
+    store("y", T.oc[:, 4 * H:4 * C], cols("qx", H, C).bitcast(dt.uint8), ("qx", H, C))
     evacuate("s", cols("yb", H, C), ("yb", H, C), 0)
     store("s", T.y[:, H:C], cols("yb", H, C), ("yb", H, C))
     store("y", T.oc[:, 0:4 * H], cols("qx", 0, H).bitcast(dt.uint8), ("qx", 0, H))

@@ -20,9 +20,9 @@ SCRATCH = {
     "qz": ("sbuf", [128, C], MX), "qzs": ("sbuf", [128, C], U8),
     "qu": ("sbuf", [128, H], MX), "qus": ("sbuf", [128, H], U8),
     "ps": ("psum", [128, 4096], F32),
-    "slo": ("sbuf", [128, H], F32), "sw": ("sbuf", [128, CODES], BF), "gs": ("sbuf", [128, C], BF), "sc": ("sbuf", [128, H + C], BF),
+    "slo": ("sbuf", [128, H], F32), "sw": ("sbuf", [128, CODES], BF), "gs": ("sbuf", [128, C], BF), "sc": ("sbuf", [128, 2 * C], BF),
     "mli": ("sbuf", [128, 20], I32), "wk": ("sbuf", [128, 20], F32), "kf": ("sbuf", [128, 20], F32),
-    "kb": ("sbuf", [128, 20], F32), "mm": ("sbuf", [128, 20], U16), "cc": ("sbuf", [128, 30], F32), "kc": ("sbuf", [128, 40], F32),
+    "kb": ("sbuf", [128, 40], F32), "mm": ("sbuf", [128, 20], U16), "kc": ("sbuf", [128, 40], F32),
     "pq": ("sbuf", [128, 40], F32), "nf": ("sbuf", [128, 20], F32), "ka": ("sbuf", [128, 60], F32),
     "mlp": ("sbuf", [128, 20], I32), "pkb": ("sbuf", [128, 40], F32), "msg": ("sbuf", [128, 40], BF), "msp": ("sbuf", [128, 40], BF),
     "ident": ("sbuf", [128, H], BF), "tab": ("sbuf", [128, WIN], BF), "gw": ("sbuf", [128, WIN], BF),
@@ -30,9 +30,9 @@ SCRATCH = {
     "su": ("sbuf", [128, H], BF), "ssu": ("sbuf", [128, H], BF), "stu": ("sbuf", [128, 10], U16),
     "cf": ("sbuf", [128, C], BF), "csc": ("sbuf", [128, C], BF), "zo": ("sbuf", [128, 20], U16),
     "fin": ("sbuf", [128, CODES], F32), "mof": ("sbuf", [128, C], F32), "yb": ("sbuf", [128, C], F32),
-    "d0": ("sbuf", [128, C], BF), "ds": ("sbuf", [128, 16], F32), "d1": ("sbuf", [128, 16], F32), "d2": ("sbuf", [128, 16], F32), "tcol": ("sbuf", [128, 16], F32),
-    "pix": ("sbuf", [128, 20], I32), "qi": ("sbuf", [128, 20], I32), "qo": ("sbuf", [128, 20], U16), "qf": ("sbuf", [128, 1], F32), "q1": ("sbuf", [128, 1], F32),
-    "e0": ("sbuf", [128, H], BF), "es": ("sbuf", [128, 16], F32), "col": ("sbuf", [128, 8], F32),
+    "d0": ("sbuf", [128, C], BF), "ds": ("sbuf", [128, 16], F32), "d1": ("sbuf", [128, 16], F32), "d2": ("sbuf", [128, 16], F32), "tcol": ("sbuf", [128, 16], I32),
+    "pix": ("sbuf", [128, 20], I32), "qi": ("sbuf", [128, 20], I32), "qo": ("sbuf", [128, 20], U16), "qf": ("sbuf", [128, 1], F32), "tm": ("sbuf", [128, 16], I32),
+    "e0": ("sbuf", [128, C], BF), "es": ("sbuf", [128, 16], F32), "col": ("sbuf", [128, 8], F32),
     "uli": ("sbuf", [128, 8], I32), "ul": ("sbuf", [128, 8], U16),
 }
 for _b in range(4):
@@ -52,7 +52,13 @@ for _r in range(3):
     SEMAPHORES += ["arrl%d" % _r, "arrc%d" % _r]
 
 LO, UP = (H, C), (0, H)
-BB, BM, INV, S_OWN, S_CUT, S_FAR, B_OWN, B_FAR = range(8)
+CUT = 128
+P1, P2 = (CUT, C), (0, CUT)
+JUMPS = [(1, 0), (1, 0), (2, 0), (3, 0), (5, 0), (8, 4), (13, 4), (13, 4), (34, 4)]
+CODES_FIRST = False
+TWIST = 6
+UNIT = 4 * TOP
+BB, INV, S_OWN, S_CUT, S_FAR = range(5)
 
 
 def rank_program(g, core, T, topo):
@@ -91,7 +97,7 @@ def rank_program(g, core, T, topo):
                 if e[6] and meets(e, r): need.add((e[3], e[4]))
         for r in writes:
             for e in log.get(r[0], []):
-                if meets(e, r) and (e[6] or e[5] != q): need.add((e[3], e[4]))
+                if meets(e, r): need.add((e[3], e[4]))
         hold(q, [(s, v) for s, v in need if known[q].get(s, 0) < v])
 
     def record(q, reads, writes, s, v):
@@ -157,15 +163,17 @@ def rank_program(g, core, T, topo):
     def line(out, in_, scale, bias, reads, writes):
         do("s", lambda q: q.activation(out, in_, SAME, bias=bias, scale=scale), reads, writes)
 
-    def pick(q, name, o, win, wn, off, a, n=10):
-        f = vcopy if q == "v" else scopy
-        f(cols(name, o, o + 16 * n), T[win][:, 0:wn].indirect(T[off][:, a:a + n]), [(win, 0, wn), (off, a, a + n)], [(name, o, o + 16 * n)])
+    def pick(q, name, o, win, wn, off, a, n=10, scale=1.0):
+        out, in_, reads, writes = cols(name, o, o + 16 * n), T[win][:, 0:wn].indirect(T[off][:, a:a + n]), [(win, 0, wn), (off, a, a + n)], [(name, o, o + 16 * n)]
+        if q == "s": scopy(out, in_, reads, writes, scale)
+        elif scale == 1.0: vcopy(out, in_, reads, writes)
+        else: ts(out, in_, scale, None, op.mult, None, reads, writes)
 
     def scan(out, src, n):
         do("v", lambda q: q.tensor_tensor_scan(cols(out, 0, n), cols("d0", 0, n), cols(src, 0, n), 0.0, op.mult, op.max), [("d0", 0, C), (src, 0, n)], [(out, 0, n)])
 
-    def scan_bits(a, src, region):
-        do("v", lambda q: q.tensor_tensor_scan(cols("sc", a, a + H), T.e0[:], src, 0.0, op.add, op.min), [("e0", 0, H), region], [("sc", a, a + H)])
+    def scan_bits(a, n, src, region):
+        do("v", lambda q: q.tensor_tensor_scan(cols("sc", a, a + n), cols("e0", 0, n), src, 0.0, op.add, op.min), [("e0", 0, n), region], [("sc", a, a + n)])
 
     def entries(out, src, n):
         ts(cols(out, 0, n // 16), T[src][:, 15:n:16], col(INV), -1.0, op.mult, op.add, [(src, 0, n), ("col", INV, INV + 1)], [(out, 0, n // 16)])
@@ -181,70 +189,68 @@ def rank_program(g, core, T, topo):
         do("t", lambda q: q.matmul_mx(psum(bank, n), T[w][:, wa:wa + 128], T[ws][:, wa:wa + 128], T[x][:, a:a + n], T[xs][:, a:a + n], True, True),
            [(w, wa, wa + 128), (ws, wa, wa + 128), (x, a, a + n), (xs, a, a + n)], [("bank%d" % bank, 0, 512)])
 
-    def evacuate(q, out, oreg, bank, scale=1.0):
-        if q == "s": scopy(out, psum(bank, H), [("bank%d" % bank, 0, 512)], [oreg], scale)
-        else: ts(out, psum(bank, H), scale, None, op.mult, None, [("bank%d" % bank, 0, 512)], [oreg])
+    def evacuate(q, out, oreg, bank, scale=1.0, a=0, n=H):
+        src = T.ps[:, 512 * bank + a:512 * bank + a + n]
+        if q == "s": scopy(out, src, [("bank%d" % bank, 0, 512)], [oreg], scale)
+        else: ts(out, src, scale, None, op.mult, None, [("bank%d" % bank, 0, 512)], [oreg])
 
     def load(q, out, in_, region, sem):
         do(q, lambda e: e.dma_start(out, in_), [], [region], sem)
 
-    load("s", T.mli[:], T.ml[:], ("mli", 0, 20), "ldm")
     load("s", T.ut[:], T.u[:], ("ut", 0, 128), "ldu")
-    load("y", cols("x0", 4 * H, 4 * C), T.x[:, 4 * H:4 * C], ("x0", H, C), "ldxl")
-    load("y", cols("x0", 0, 4 * H), T.x[:, 0:4 * H], ("x0", 0, H), "ldxu")
+    load("s", T.mli[:], T.ml[:], ("mli", 0, 20), "ldm")
+    load("y", cols("x0", 4 * CUT, 4 * C), T.x[:, 4 * CUT:4 * C], ("x0", CUT, C), "ldxl")
+    load("y", cols("x0", 0, 4 * CUT), T.x[:, 0:4 * CUT], ("x0", 0, CUT), "ldxu")
     load("y", T.wq[:].bitcast(dt.uint8), T.wc[:], ("wq", 0, 512), "ldw")
     load("y", T.wqs[:], T.ws[:], ("wqs", 0, 512), "ldws")
     load("y", T.vt[:], T.v[:], ("vt", 0, 128), "ldv")
 
     do("v", lambda q: q.memset(T.eo[:], 1.0), [], [("eo", 0, 528)])
+    do("g", lambda q: q.iota(T.tcol[:], [[1, 16]], 128, -1), [], [("tcol", 0, 16)])
     do("g", lambda q: q.iota(T.pix[:], [[0, 20]], 0, 1), [], [("pix", 0, 20)])
-    do("g", lambda q: q.iota(T.tcol[:], [[1, 16]], 0, 0, allow_small_or_imprecise_dtypes=True), [], [("tcol", 0, 16)])
     do("g", lambda q: q.iota(T.uli[:], [[16, 8]], 0, 0), [], [("uli", 0, 8)])
-    do("g", lambda q: q.iota(T.ident[:], [[1, H]], 0, 0, allow_small_or_imprecise_dtypes=True), [], [("ident", 0, H)])
     do("g", lambda q: q.affine_select(T.et[:], T.eo[:], [[-1, 528]], op.is_equal, 0.0, 3, 4), [("eo", 0, 528)], [("et", 0, 528)])
+    do("g", lambda q: q.iota(T.ident[:], [[1, H]], 0, 0, allow_small_or_imprecise_dtypes=True), [], [("ident", 0, H)])
     first = T.cores[rank ^ STEP[0]]
     lanes = topo.engines(core, first)
     arrival([("mlp", 0, 20)], "arrm", len(lanes))
     arrival([("msp", 0, 40)], "arrl0", len(lanes))
     send(first, lanes, [(T.mli[:], T.mlp[:], ("mli", 0, 20))], "arrm")
-    do("v", lambda q: q.tensor_scalar(T.qi[:], T.pix[:], 15, None, op.bitwise_and), [("pix", 0, 20)], [("qi", 0, 20)])
-    vcopy(T.ul[:], T.uli[:], [("uli", 0, 8)], [("ul", 0, 8)])
-    vcopy(T.qf[:], cols("qi", 0, 1), [("qi", 0, 1)], [("qf", 0, 1)])
+    ts(T.tm[:], T.tcol[:], 15, None, op.bitwise_and, None, [("tcol", 0, 16)], [("tm", 0, 16)])
+    ts(T.qi[:], T.pix[:], 15, None, op.bitwise_and, None, [("pix", 0, 20)], [("qi", 0, 20)])
+    ts(T.d2[:], T.tm[:], 0.0, -1.0, op.is_equal, op.mult, [("tm", 0, 16)], [("d2", 0, 16)])
+    ts(T.d1[:], T.tm[:], 1.0, TOP - 1.0, op.is_equal, op.mult, [("tm", 0, 16)], [("d1", 0, 16)])
     vcopy(T.qo[:], T.qi[:], [("qi", 0, 20)], [("qo", 0, 20)])
-    ts(T.q1[:], T.qf[:], 1.0, None, op.add, None, [("qf", 0, 1)], [("q1", 0, 1)])
-    ts(T.d2[:], T.tcol[:], T.qf[:, 0:1], -1.0, op.is_equal, op.mult, [("tcol", 0, 16), ("qf", 0, 1)], [("d2", 0, 16)])
-    ts(col(BB), T.qf[:], 14.5, 2.0, op.is_lt, op.mult, [("qf", 0, 1)], [("col", BB, BB + 1)])
-    ts(T.d1[:], T.tcol[:], T.q1[:, 0:1], TOP - 1.0, op.is_equal, op.mult, [("tcol", 0, 16), ("q1", 0, 1)], [("d1", 0, 16)])
-    ts(col(INV), T.qf[:], 14.5, 1.0 / TOP, op.is_gt, op.max, [("qf", 0, 1)], [("col", INV, INV + 1)])
+    ts(col(INV), cols("qi", 0, 1), 14.5, 1.0 / TOP, op.is_gt, op.max, [("qi", 0, 1)], [("col", INV, INV + 1)])
     tt(T.ds[:], T.d2[:], T.d1[:], op.add, [("d2", 0, 16), ("d1", 0, 16)], [("ds", 0, 16)])
-    ts(col(BM), col(BB), -1.0, None, op.add, None, [("col", BB, BB + 1)], [("col", BM, BM + 1)])
+    ts(T.qf[:], cols("qi", 0, 1), 14.5, 4.0, op.is_lt, op.mult, [("qi", 0, 1)], [("qf", 0, 1)])
+    vcopy(T.ul[:], T.uli[:], [("uli", 0, 8)], [("ul", 0, 8)])
     ts(T.es[:], T.ds[:], 0.25, -8.0, op.min, op.mult, [("ds", 0, 16)], [("es", 0, 16)])
+    ts(col(BB), T.qf[:], -1.0, None, op.add, None, [("qf", 0, 1)], [("col", BB, BB + 1)])
+    scopy(cols("e0", 0, C - 16 * TWIST), T.es[:].indirect(T.qo[:, TWIST:20]), [("es", 0, 16), ("qo", 0, 20)], [("e0", 0, C)])
     line(T.d0[:], T.ds[:].indirect(T.qo[:, 0:20]), 1.0, 1.0, [("ds", 0, 16), ("qo", 0, 20)], [("d0", 0, C)])
-    scopy(T.e0[:], T.es[:].indirect(T.qo[:, 0:10]), [("es", 0, 16), ("qo", 0, 10)], [("e0", 0, H)])
-    for k, src, scale, bias in ((S_OWN, INV, 1.0 / (OWN[1] * TOP), 0.0), (S_CUT, INV, -2.0, 0.0), (S_FAR, INV, 1.0 / (FAR[1] * TOP), 0.0),
-                                (B_OWN, BB, 1.0, -OWN[0] / (OWN[1] * TOP)), (B_FAR, BB, 1.0, -FAR[0] / (FAR[1] * TOP))):
-        line(col(k), col(src), scale, bias, [("col", src, src + 1)], [("col", k, k + 1)])
+    for k, scale in ((S_OWN, 1.0 / (OWN[1] * UNIT)), (S_CUT, -2.0), (S_FAR, 1.0 / (FAR[1] * UNIT))):
+        scopy(col(k), col(INV), [("col", INV, INV + 1)], [("col", k, k + 1)], scale)
 
-    def table(out, region, code):
-        ts(out, T.ident[:], float(code[1]), float(code[0]), op.mult, op.add, [("ident", 0, H)], [region])
-
-    table(cols("tab", 0, H), ("tab", 0, H), (1, 1))
-    table(cols("gw", 0, H), ("gw", 0, H), FAR)
-    for w in ("tab", "wb"):
-        table(cols(w, TOP, WIN), (w, TOP, WIN), OWN)
-    for w in ("wa", "wb"):
-        for code in (OWN, FAR):
-            table(*spots(w, code), code)
+    def table(q, out, region, code):
+        if q == "v": ts(out, T.ident[:], float(code[1]), float(code[0]), op.mult, op.add, [("ident", 0, H)], [region])
+        else: line(out, T.ident[:], float(code[1]), float(code[0]), [("ident", 0, H)], [region])
 
     def unit(b):
         do("v", lambda q: q.quantize_mx(cols("eq", 128 * b, 128 * b + 128), cols("eqs", 128 * b, 128 * b + 128), cols("et", 3 - b, 515 - b)),
            [("et", 0, 528)], [("eq", 128 * b, 128 * b + 128), ("eqs", 128 * b, 128 * b + 128)])
 
-    def scores(half):
-        product(0 if half == LO else 4, "u2", "u2s", 0, "qx", "qxs", half[0], H)
+    def scores(part, w="u2", ws="u2s"):
+        product(0 if part == P1 else 4, w, ws, 0, "qx", "qxs", part[0], part[1] - part[0])
 
-    def state_quant(x, half):
-        quant("qx", "qxs", x, half[0], H, half[0])
+    def state_quant(x, part):
+        quant("qx", "qxs", x, part[0], part[1] - part[0], part[0])
+
+    def compare(r, part):
+        a, e, bank, at = (CUT, H, 0, 0) if part == P1 else (0, CUT, 4, 0)
+        for code, o in ((FAR if r else (H + 1, 1), op.is_gt), (OWN if r else (1, 1), op.is_le)):
+            lo, hi = code[0] - 1 + code[1] * a, code[0] - 1 + code[1] * e
+            tt(T.sw[:, lo:hi:code[1]], psum(bank, e - a), cols("slo", a, e), o, [("bank%d" % bank, 0, 512), ("slo", a, e)], [("sw", lo, hi)])
 
     def address(half):
         return (0, H) if half == LO else (TOP, WIN)
@@ -254,53 +260,54 @@ def rank_program(g, core, T, topo):
         scopy(cols("xp%d" % b, a, e), T[x][:, 4 * half[0] + b:4 * half[1]:4], [(x, half[0], half[1], b)], [("xp%d" % b, a, e)])
 
     def scores_low_out():
-        evacuate("s", T.slo[:], ("slo", 0, H), 0)
+        evacuate("s", T.slo[:], ("slo", 0, H), 0, 1.0, H - CUT)
 
-    def places(m, outs):
+    def places(m, out):
         return [lambda: ts(T.wk[:], T[m][:], H - 0.5, -float(H), op.is_gt, op.mult, [(m, 0, 20)], [("wk", 0, 20)]),
                 lambda: tt(T.kf[:], T[m][:], T.wk[:], op.add, [(m, 0, 20), ("wk", 0, 20)], [("kf", 0, 20)]),
-                lambda: [ts(out, T.kf[:], 1.0 / TOP, col(BB), op.mult, op.add, [("kf", 0, 20), ("col", BB, BB + 1)], [region]) for out, region in outs]]
+                lambda: (ts(cols(out, 0, 20), T.kf[:], 1.0 / UNIT, None, op.mult, None, [("kf", 0, 20)], [(out, 0, 20)]),
+                         ts(cols(out, 20, 40), T.kf[:], 1.0 / UNIT, col(BB), op.mult, op.add, [("kf", 0, 20), ("col", BB, BB + 1)], [(out, 20, 40)]))]
 
-    def choose():
-        for k, c, f in ((10, BM, 4.0), (20, BB, -4.0), (0, BB, -4.0)):
-            ts(cols("cc", k, k + 10), T.sc[:, 15:H:16], col(c), f, op.add, op.mult, [("sc", 0, H), ("col", c, c + 1)], [("cc", k, k + 10)])
+    swaps, halves = T.sc[:, 15:C:16], T.sc[:, C + 15:2 * C:16]
 
-    def blend():
-        for k in (10, 0):
-            tt(cols("kc", 2 * k, 2 * k + 20), cols("cc", k, k + 20), T.kb[:], op.add, [("cc", k, k + 20), ("kb", 0, 20)], [("kc", 2 * k, 2 * k + 20)])
+    def swapped(out, src, region):
+        for k, o in ((0, op.subtract), (20, op.add)):
+            tt(cols(out, k, k + 20), src(k), swaps, o, [region(k), ("sc", 0, C)], [(out, k, k + 20)])
 
-    def offers(out, add, a):
-        for w in (1, 0):
-            tt(T[out][:, w:40:2], T.sc[:, H + 15:3 * H:16], cols(add, a * w, a * w + 20), op.add, [("sc", H, 3 * H), (add, a * w, a * w + 20)], [(out, 0, 40, w)])
+    def offers():
+        for k in (0, 20):
+            tt(cols("pq", k, k + 20), halves, cols("kc", k, k + 20), op.add, [("sc", C, 2 * C), ("kc", k, k + 20)], [("pq", k, k + 20)])
 
     def larger():
-        tt(T.nf[:], cols("pq", 0, 20), cols("pq", 20, 40), op.max, [("pq", 0, 40)], [("nf", 0, 20)])
+        for k in (0, 10):
+            tt(cols("nf", k, k + 10), cols("pq", k, k + 10), cols("pq", 30 - k, 40 - k), op.max, [("pq", 0, 40)], [("nf", k, k + 10)])
 
     def addresses(out):
-        for w in (1, 0):
-            ts(cols(out, 10 * w, 10 * w + 10), T.nf[:, w:20:2], float(TOP), None, op.mult, None, [("nf", 0, 20)], [(out, 10 * w, 10 * w + 10)])
+        ts(T[out][:], T.nf[:], float(UNIT), None, op.mult, None, [("nf", 0, 20)], [(out, 0, 20)])
 
-    steps = places("mli", [(T.kb[:], ("kb", 0, 20))])
-    steps[0]()
-    vcopy(T.mm[:], T.mli[:], [("mli", 0, 20)], [("mm", 0, 20)])
+    steps = places("mli", "kb")
     unit(0)
-    steps[1]()
     unit(1)
-    steps[2]()
     quant("uq", "uqs", "ut", 0, 128)
-    state_quant("x0", LO)
+    unit(2)
     do("v", lambda q: q.tensor_copy(T.u2[:, 0:128].bitcast(dt.uint32), T.uq[:, 0:128].bitcast(dt.uint32).indirect(T.ul[:, 0:8])),
        [("uq", 0, 128), ("ul", 0, 8)], [("u2", 0, 128)])
     scopy(T.u2s[:, 0:128], T.uqs[:, 0:128].indirect(T.ul[:, 0:8]), [("uqs", 0, 128), ("ul", 0, 8)], [("u2s", 0, 128)])
-    scores(LO)
-    state_quant("x0", UP)
-    scores(UP)
+    state_quant("x0", P1)
+    scores(P1)
+    steps[0]()
+    vcopy(T.mm[:], T.mli[:], [("mli", 0, 20)], [("mm", 0, 20)])
+    plane("x0", 0, LO)
     scores_low_out()
-    unit(2)
-    unit(3)
-    planes = [(b, half) for b in range(4) for half in (UP, LO)]
-    for b, half in planes[:3]:
-        plane("x0", b, half)
+    steps[1]()
+    state_quant("x0", P2)
+    scores(P2)
+    steps[2]()
+    compare(0, P1)
+    for b in range(1, 4):
+        plane("x0", b, LO)
+    table("s", cols("tab", 0, H), ("tab", 0, H), (1, 1))
+    table("s", cols("tab", TOP, WIN), ("tab", TOP, WIN), OWN)
 
     for r in range(3):
         last = r == 2
@@ -312,29 +319,37 @@ def rank_program(g, core, T, topo):
         if r: arrival([(npl, 0, 20)], "arrl%d" % r, len(engines))
         arrival([(pl, 0, H), (pls, 0, H)], "arrc%d" % r, 2 * len(engines))
 
-        upper, lower = (spots("sw", OWN), spots("sw", FAR)) if r else ((cols("sw", 0, H), ("sw", 0, H)), (cols("sw", H, C), ("sw", H, C)))
         mates = "zo" if r else "mm"
-        for (view, region), o in ((lower, op.is_gt), (upper, op.is_le)):
-            tt(view, psum(4, H), T.slo[:], o, [("bank4", 0, 512), ("slo", 0, H)], [region])
-        pick("s", "gs", H, "sw", CODES, mates, 10)
-        pick("s", "gs", 0, "sw", CODES, mates, 0)
+        compare(r, P2)
+        pick("s", "gs", 16 * TWIST, "sw", CODES, mates, TWIST, 20 - TWIST, 0.25)
         if r == 0:
-            for b, half in planes[3:]:
-                plane("x0", b, half)
-        scan_bits(0, *lower)
-        if r == 1: quant("vq", "vqs", "vt", 0, 128)
-        choose()
-        scan_bits(2 * H, cols("gs", H, C), ("gs", H, C))
-        blend()
-        scan_bits(H, cols("gs", 0, H), ("gs", 0, H))
+            for b in range(4):
+                plane("x0", b, UP)
+        for a in (0, H):
+            scan_bits(a, H, *spots("sw", FAR if r else (H + 1, 1)))
+        pick("v", "gs", 0, "sw", CODES, mates, 0, TWIST, 0.25)
+        swapped("kc", lambda k: cols("kb", k, k + 20), lambda k: ("kb", k, k + 20))
+        for a, e in ((0, 16 * TWIST), (16 * TWIST, C)):
+            scan_bits(C + a, e - a, cols("gs", a, e), ("gs", a, e))
+        if r == 0: unit(3)
         if r == 0:
-            offers("msg", "cc", 10)
+            swapped("msg", lambda k: halves, lambda k: ("sc", C, 2 * C))
             send(partner, engines, [(T.msg[:], T.msp[:], ("msg", 0, 40))], "arrl0")
-        offers("pq", "kc", 20)
+        steps = places("mlp", "pkb") if r == 0 else [lambda: None] * 3
+        offers()
+        steps[0]()
         larger()
+        steps[1]()
         addresses(nl)
+        steps[2]()
         if r: send(partner, engines, [(T[nl][:], T[npl][:], (nl, 0, 20))], "arrl%d" % r)
         pick("s", "gw", TOP, "tab", WIN, nl, 10)
+        if r == 0:
+            table("s", cols("gw", 0, H), ("gw", 0, H), FAR)
+            for w in ("wa", "wb"):
+                for code in (OWN, FAR):
+                    table("s", *spots(w, code), code)
+            table("s", cols("wb", TOP, WIN), ("wb", TOP, WIN), OWN)
 
         def total(half, b, c=0, d=10):
             xp = "xp%d" % b
@@ -362,24 +377,27 @@ def rank_program(g, core, T, topo):
         def unpacked(q, b, k, code):
             evacuate(q, *spots("b%d" % b, code), k + b)
 
-        steps = places("mlp", [(T.pkb[:, w:40:2], ("pkb", 0, 40, w)) for w in range(2)])
         for b in range(4):
+            if r == 0 and b == 3: tt(T.pq[:], T.msp[:], T.pkb[:], op.add, [("msp", 0, 40), ("pkb", 0, 40)], [("pq", 0, 40)])
             total(LO, b)
-            if r == 0 and b < 3: steps[b]()
-        total(UP, 0, 0, 4)
+        away = CODES_FIRST and topo.chip(core) != topo.chip(partner)
+        if r == 0: larger()
+        total(UP, 0, 0, 4 if away else 10)
+        if r == 0: addresses(npl)
         quant("qz", "qzs", "z", H, H, H)
         layer(0, LO)
-        if r == 0: tt(T.pq[:], T.msp[:], T.pkb[:], op.add, [("msp", 0, 40), ("pkb", 0, 40)], [("pq", 0, 40)])
-        total(UP, 0, 4, 10)
-        if r == 0: larger()
-        total(UP, 1, 0, 4)
-        if r == 0: addresses(npl)
-        total(UP, 1, 4, 10)
+        if away:
+            total(UP, 0, 4, 10)
+            total(UP, 1, 0, 4)
+            for b in range(4):
+                made("sv"[b % 2], b, 0, LO)
+            total(UP, 1, 4, 10)
+            low_codes()
+        else: total(UP, 1, 0, 4)
 
         pick("s", "wa", 0, "gw", WIN, npl, 0)
         pick("s", "su", 0, "gw", WIN, npl, 10)
-        made("s", 0, 0, LO)
-        made("s", 1, 0, LO)
+        if not away: made("s", 0, 0, LO)
 
         def upper_layer():
             quant("qz", "qzs", "z", 0, H)
@@ -387,82 +405,92 @@ def rank_program(g, core, T, topo):
 
         def upper_codes():
             quant("qu", "qus", "a", 0, H)
-            unpack(0, "qu", "qus")
-            unpack(4, pl, pls)
+            unpack(4, "qu", "qus")
+            unpack(0, pl, pls)
 
-        behind_scan = {0: lambda: total(UP, 2, 0, 4), 1: lambda: total(UP, 3, 0, 4), 2: upper_layer, 3: lambda: entries("stu", "ssu", H),
-                       4: lambda: made("v", 1, 4, UP), 5: upper_codes, 7: lambda: unpacked("v", 1, 0, OWN)}
-        behind_list = {0: lambda: (made("v", 2, 0, LO), made("v", 3, 0, LO), total(UP, 2, 4, 10), low_codes()), 1: lambda: total(UP, 3, 4, 10),
-                       2: lambda: scan("ssu", "su", H), 3: lambda: made("v", 0, 4, UP), 4: lambda: made("v", 3, 4, UP), 6: lambda: unpacked("v", 0, 0, OWN),
-                       7: lambda: [unpacked("v", b, 0, OWN) for b in range(2, 4)]}
-        behind_pick = {4: lambda: made("s", 2, 4, UP)}
-        win, nxt = "wa", "wb"
-        for k in range(9):
-            if k < 8:
-                scn, lu = "scn%d" % (k % 3), "lu%d" % (k % 3)
-                scan(scn, win, H)
-                if k in behind_scan: behind_scan[k]()
+        behind_scan = {0: lambda: total(UP, 1, 4, 10), 1: low_codes, 2: lambda: total(UP, 2, 4, 10), 3: lambda: total(UP, 3, 4, 10), 4: upper_layer}
+        behind_list = {0: lambda: [made("v", b, 0, LO) for b in range(1, 4)], 1: lambda: total(UP, 2, 0, 4), 2: lambda: total(UP, 3, 0, 4),
+                       3: lambda: scan("ssu", "su", H), 4: lambda: entries("stu", "ssu", H), 5: lambda: made("v", 1, 4, UP),
+                       6: lambda: made("v", 2, 4, UP), 7: upper_codes}
+        behind_pick = {5: lambda: made("s", 0, 4, UP), 6: lambda: made("s", 3, 4, UP)}
+        if away:
+            behind_scan = {0: lambda: total(UP, 2, 0, 4), 1: lambda: total(UP, 3, 4, 10), 2: upper_layer, 3: lambda: entries("stu", "ssu", H)}
+            behind_list = {0: lambda: (total(UP, 2, 4, 10), total(UP, 3, 0, 4)), 2: lambda: scan("ssu", "su", H),
+                           3: lambda: made("v", 0, 4, UP), 4: lambda: made("v", 2, 4, UP), 5: upper_codes}
+            behind_pick = {3: lambda: made("s", 1, 4, UP), 4: lambda: made("s", 3, 4, UP)}
+        win, nxt, power, lists = "wa", "wb", 1, {}
+        for k, (by, share) in enumerate(JUMPS):
+            def step(q, c, d): pick(q, nxt, 16 * c, win, CODES, lists[by], c, d - c)
+            fresh = power in [j for j, _ in JUMPS]
+            if k: step("s", share, 10)
+            if k in behind_pick: behind_pick[k]()
+            scn, lu = "scn%d" % (k % 3), "lu%d" % (k % 3)
+            if fresh: scan(scn, win, H)
+            if share: step("v", 0, share)
+            if k in behind_scan: behind_scan[k]()
+            if fresh:
                 entries(lu, scn, H)
-            if k == 4: behind_pick[k]()
+                lists[power] = lu
+            if k == 0: step("s", 0, 10)
             if k in behind_list: behind_list[k]()
-            pick("s", nxt, 0, win, CODES, "lu%d" % (max(k - 1, 0) % 3), 0)
-            win, nxt = nxt, win
+            win, nxt, power = nxt, win, power + by
+        if r == 0: quant("vq", "vqs", "vt", 0, 128)
         pick("v", "cf", 0, win, WIN, nl, 0)
         pick("s", "cf", H, win, CODES, "stu", 0)
-        for b in range(4):
-            unpacked("s", b, 4, FAR)
+        unpacked("v", 0, 4, OWN)
         scan("csc", "cf", C)
+        unpacked("v", 1, 4, OWN)
         entries("zo", "csc", C)
+        for b in range(4):
+            if b > 1: unpacked("s", b, 4, OWN)
+            unpacked("s", b, 0, FAR)
 
-        def renew(half, b):
-            a, e = address(half)
-            o = 10 if half == LO else 0
-            xp, bb = "xp%d" % b, "b%d" % b
-            tt(T[xn][:, 4 * half[0] + b:4 * half[1]:4], T[bb][:, 0:CODES].indirect(T.zo[:, o:o + 10]), cols(xp, a, e), op.add,
-               [(bb, 0, CODES), ("zo", o, o + 10), (xp, a, e)], [(xn, half[0], half[1], b)])
+        def renew(part, b):
+            bb = "b%d" % b
+            lo, hi = part
+            tt(T[xn][:, 4 * lo + b:4 * hi:4], T[bb][:, 0:CODES].indirect(T.zo[:, lo // 16:hi // 16]), T[x][:, 4 * lo + b:4 * hi:4], op.add,
+               [(bb, 0, CODES), ("zo", lo // 16, hi // 16), (x, lo, hi, b)], [(xn, lo, hi, b)])
 
         if not last:
-            for k, (s, b) in enumerate(((S_OWN, col(B_OWN)), (S_CUT, 2.0 * (FAR[0] - 6)), (S_FAR, col(B_FAR)))):
-                line(cols("ka", 20 * k, 20 * k + 20), T.csc[:, 15:C:16], col(s), b, [("csc", 0, C), ("col", 0, 8)], [("ka", 20 * k, 20 * k + 20)])
+            for k, (s, b) in enumerate(((S_OWN, -OWN[0] / (OWN[1] * UNIT)), (S_CUT, 2.0 * (FAR[0] - 6)), (S_FAR, -FAR[0] / (FAR[1] * UNIT)))):
+                line(cols("ka", 20 * k, 20 * k + 20), T.csc[:, 15:C:16], col(s), b, [("csc", 0, C), ("col", s, s + 1)], [("ka", 20 * k, 20 * k + 20)])
         else:
             for code, first_column in ((OWN, 0.0), (FAR, float(H))):
                 view, region = spots("fin", code)
                 line(view, T.ident[:], 1.0, first_column, [("ident", 0, H)], [region])
             pick("s", "mof", 0, "fin", CODES, "zo", 0, 20)
         for b in range(4):
-            renew(LO, b)
+            renew(P1 if b else (0, C), b)
             if not last: plane(xn, b, LO)
-        renew(UP, 0)
-        state_quant(xn, LO)
-        if not last: scores(LO)
-        else: product(0, "vq", "vqs", 0, "qx", "qxs", H, H)
-        for b in range(1, 4):
-            renew(UP, b)
+        renew(P2, 1)
+        state_quant(xn, P1)
+        if not last:
+            scores(P1)
+            scores_low_out()
+        else: scores(P1, "vq", "vqs")
+        for b in range(2, 4):
+            renew(P2, b)
         if not last:
             tt(T.kf[:], cols("ka", 0, 20), cols("ka", 20, 40), op.min, [("ka", 0, 40)], [("kf", 0, 20)])
-        state_quant(xn, UP)
+        state_quant(xn, P2)
         if not last:
-            tt(T.kb[:], T.kf[:], cols("ka", 40, 60), op.max, [("kf", 0, 20), ("ka", 40, 60)], [("kb", 0, 20)])
-            scores(UP)
-            plane(xn, 0, UP)
-            plane(xn, 1, UP)
-            scores_low_out()
-            plane(xn, 2, UP)
-            plane(xn, 3, UP)
-        else:
-            product(4, "vq", "vqs", 0, "qx", "qxs", 0, H)
+            scores(P2)
+            tt(cols("kb", 0, 20), T.kf[:], cols("ka", 40, 60), op.max, [("kf", 0, 20), ("ka", 40, 60)], [("kb", 0, 20)])
+            compare(r + 1, P1)
+            ts(cols("kb", 20, 40), cols("kb", 0, 20), col(BB), None, op.add, None, [("kb", 0, 20), ("col", BB, BB + 1)], [("kb", 20, 40)])
+            for b in range(4):
+                plane(xn, b, UP)
+        else: scores(P2, "vq", "vqs")
 
     def store(q, out, in_, region):
         do(q, lambda e: e.dma_start(out, in_), [region], [], "outs")
 
     store("y", T.mo[:], T.mof[0:128:16, :], ("mof", 0, C))
-    store("y", T.oc[:, 4 * H:4 * C], cols("qx", H, C).bitcast(dt.uint8), ("qx", H, C))
-    evacuate("s", cols("yb", H, C), ("yb", H, C), 0)
-    store("s", T.y[:, H:C], cols("yb", H, C), ("yb", H, C))
-    store("y", T.oc[:, 0:4 * H], cols("qx", 0, H).bitcast(dt.uint8), ("qx", 0, H))
+    for (lo, hi), bank in ((P1, 0), (P2, 4)):
+        store("y", T.oc[:, 4 * lo:4 * hi], cols("qx", lo, hi).bitcast(dt.uint8), ("qx", lo, hi))
+        evacuate("s", cols("yb", lo, hi), ("yb", lo, hi), bank, 1.0, 0, hi - lo)
+        store("s", T.y[:, lo:hi], cols("yb", lo, hi), ("yb", lo, hi))
     for k in range(4):
         store("y", T.osc[4 * k:4 * k + 4, :], T.qxs[32 * k:32 * k + 4, 0:C], ("qxs", 0, C))
-    evacuate("s", cols("yb", 0, H), ("yb", 0, H), 4)
-    store("s", T.y[:, 0:H], cols("yb", 0, H), ("yb", 0, H))
     for s in SEMAPHORES:
         if count.get(s, 0): g.wait_ge(T.sem[s], count[s])

@@ -20,11 +20,12 @@ SCRATCH = {
     "qz": ("sbuf", [128, C], MX), "qzs": ("sbuf", [128, C], U8),
     "qu": ("sbuf", [128, H], MX), "qus": ("sbuf", [128, H], U8),
     "ps": ("psum", [128, 4096], F32),
-    "slo": ("sbuf", [128, H], F32), "sw": ("sbuf", [128, CODES], BF), "gs": ("sbuf", [128, C], BF), "sc": ("sbuf", [128, 2 * C], BF),
+    "slo": ("sbuf", [128, H], F32), "sw": ("sbuf", [128, CODES], BF), "gs": ("sbuf", [128, C], BF), "sc": ("sbuf", [128, 512], BF),
     "mli": ("sbuf", [128, 20], I32), "wk": ("sbuf", [128, 20], F32), "kf": ("sbuf", [128, 20], F32),
-    "kb": ("sbuf", [128, 40], F32), "mm": ("sbuf", [128, 20], U16), "kc": ("sbuf", [128, 40], F32),
-    "pq": ("sbuf", [128, 40], F32), "nf": ("sbuf", [128, 20], F32), "ka": ("sbuf", [128, 60], F32),
-    "mlp": ("sbuf", [128, 20], I32), "pkb": ("sbuf", [128, 40], F32), "msg": ("sbuf", [128, 40], BF), "msp": ("sbuf", [128, 40], BF),
+    "kb": ("sbuf", [128, 20], F32), "mm": ("sbuf", [128, 20], U16), "ka": ("sbuf", [128, 60], F32), "dk": ("sbuf", [128, 10], F32),
+    "yy": ("sbuf", [128, 20], F32), "ee": ("sbuf", [128, 10], F32), "dd": ("sbuf", [128, 60], F32), "rr": ("sbuf", [128, 60], F32),
+    "mlp": ("sbuf", [128, 20], I32), "pkb": ("sbuf", [128, 20], F32), "pk": ("sbuf", [128, 10], F32), "pd": ("sbuf", [128, 30], F32),
+    "pr": ("sbuf", [128, 30], F32), "msg": ("sbuf", [128, 30], BF), "msp": ("sbuf", [128, 30], BF),
     "ident": ("sbuf", [128, H], BF), "tab": ("sbuf", [128, WIN], BF), "gw": ("sbuf", [128, WIN], BF),
     "wa": ("sbuf", [128, WIN], BF), "wb": ("sbuf", [128, WIN], BF),
     "su": ("sbuf", [128, H], BF), "ssu": ("sbuf", [128, H], BF), "stu": ("sbuf", [128, 10], U16),
@@ -32,15 +33,15 @@ SCRATCH = {
     "fin": ("sbuf", [128, CODES], F32), "mof": ("sbuf", [128, C], F32), "yb": ("sbuf", [128, C], F32),
     "d0": ("sbuf", [128, C], BF), "ds": ("sbuf", [128, 16], F32), "d1": ("sbuf", [128, 16], F32), "d2": ("sbuf", [128, 16], F32), "tcol": ("sbuf", [128, 16], I32),
     "pix": ("sbuf", [128, 20], I32), "qi": ("sbuf", [128, 20], I32), "qo": ("sbuf", [128, 20], U16), "qf": ("sbuf", [128, 1], F32), "tm": ("sbuf", [128, 16], I32),
-    "e0": ("sbuf", [128, C], BF), "es": ("sbuf", [128, 16], F32), "col": ("sbuf", [128, 8], F32),
+    "e0": ("sbuf", [128, H], BF), "es": ("sbuf", [128, 16], F32), "col": ("sbuf", [128, 10], F32),
     "uli": ("sbuf", [128, 8], I32), "ul": ("sbuf", [128, 8], U16),
 }
 for _b in range(4):
     SCRATCH["xp%d" % _b] = ("sbuf", [128, WIN], BF)
     SCRATCH["b%d" % _b] = ("sbuf", [128, CODES], BF)
+    SCRATCH["scn%d" % _b] = ("sbuf", [128, H], BF)
+    SCRATCH["lu%d" % _b] = ("sbuf", [128, 10], U16)
 for _r in range(3):
-    SCRATCH["scn%d" % _r] = ("sbuf", [128, H], BF)
-    SCRATCH["lu%d" % _r] = ("sbuf", [128, 10], U16)
     SCRATCH["nl%d" % _r] = ("sbuf", [128, 20], U16)
     SCRATCH["np%d" % _r] = ("sbuf", [128, 20], U16)
     SCRATCH["ql%d" % _r] = ("sbuf", [128, H], MX)
@@ -49,16 +50,23 @@ for _r in range(3):
     SCRATCH["pls%d" % _r] = ("sbuf", [128, H], U8)
 SEMAPHORES = ["sv", "ss", "st", "sg", "sent", "outs", "ldxl", "ldxu", "ldu", "ldm", "ldw", "ldws", "ldv", "arrm"]
 for _r in range(3):
-    SEMAPHORES += ["arrl%d" % _r, "arrc%d" % _r]
+    SEMAPHORES += ["arrl%d" % _r, "arrs%d" % _r, "arrc%d" % _r]
 
 LO, UP = (H, C), (0, H)
 CUT = 128
 P1, P2 = (CUT, C), (0, CUT)
-JUMPS = [(1, 0), (1, 0), (2, 0), (3, 0), (5, 0), (8, 4), (13, 4), (13, 4), (34, 4)]
-CODES_FIRST = False
+HOME = ([(1, 0, "l0s", "z1b", "l2s z3a z2 l1v"), (1, 0, "l3s", "z3b", ""), (2, 0, "ps", "Z A", ""), (3, 4, "u0s", "", "S"), (5, 4, "u1s", "", "E"),
+         (8, 4, "u2s", "", "u3v"), (13, 4, "", "", "B"), (13, 4, "", "", ""), (34, 6, "", "", "")],
+        {"sums": "y0 y1 y2 y3 z0 Y z1a", "first": "", "ends": "o0s", "scan": "", "list": "f0s o1v o2s f1s f2s f3s o3s"})
+AWAY = ([(1, 0, "l1s l3s l2v", "z3b", "A z2 z3a"), (1, 0, "ps", "Z", ""), (2, 6, "", "", "S"), (3, 4, "u1s", "", "E"), (5, 6, "u0s", "", ""),
+         (8, 4, "u2s", "", "u3v"), (13, 4, "", "", ""), (13, 2, "B", "", ""), (34, 6, "", "o0v", "")],
+        {"sums": "y0 y1 y2 y3 z1a Y z0 z1b l0v", "first": "", "ends": "o1s", "scan": "", "list": "o2s f0s f1s f2s f3s o3s"})
+HALF = False
+AHEAD = True
+WHOLE = 1
 TWIST = 6
-UNIT = 4 * TOP
-BB, INV, S_OWN, S_CUT, S_FAR = range(5)
+UNIT, LIFT = 4 * TOP, 8.0
+INV, S_OWN, S_CUT, S_FAR, C1, CB, BM, BN, CL, CN = range(10)
 
 
 def rank_program(g, core, T, topo):
@@ -172,8 +180,8 @@ def rank_program(g, core, T, topo):
     def scan(out, src, n):
         do("v", lambda q: q.tensor_tensor_scan(cols(out, 0, n), cols("d0", 0, n), cols(src, 0, n), 0.0, op.mult, op.max), [("d0", 0, C), (src, 0, n)], [(out, 0, n)])
 
-    def scan_bits(a, n, src, region):
-        do("v", lambda q: q.tensor_tensor_scan(cols("sc", a, a + n), cols("e0", 0, n), src, 0.0, op.add, op.min), [("e0", 0, n), region], [("sc", a, a + n)])
+    def scan_bits(k, src, region):
+        do("v", lambda q: q.tensor_tensor_scan(T.sc[:, 16 * k:16 * k + 3 * H:3], T.e0[:], src, 0.0, op.add, op.min), [("e0", 0, H), region], [("sc", 0, 512, k)])
 
     def entries(out, src, n):
         ts(cols(out, 0, n // 16), T[src][:, 15:n:16], col(INV), -1.0, op.mult, op.add, [(src, 0, n), ("col", INV, INV + 1)], [(out, 0, n // 16)])
@@ -201,6 +209,7 @@ def rank_program(g, core, T, topo):
     load("s", T.mli[:], T.ml[:], ("mli", 0, 20), "ldm")
     load("y", cols("x0", 4 * CUT, 4 * C), T.x[:, 4 * CUT:4 * C], ("x0", CUT, C), "ldxl")
     load("y", cols("x0", 0, 4 * CUT), T.x[:, 0:4 * CUT], ("x0", 0, CUT), "ldxu")
+    waits("y", [full(("x0", 0, C))], [])
     load("y", T.wq[:].bitcast(dt.uint8), T.wc[:], ("wq", 0, 512), "ldw")
     load("y", T.wqs[:], T.ws[:], ("wqs", 0, 512), "ldws")
     load("y", T.vt[:], T.v[:], ("vt", 0, 128), "ldv")
@@ -209,13 +218,13 @@ def rank_program(g, core, T, topo):
     do("g", lambda q: q.iota(T.tcol[:], [[1, 16]], 128, -1), [], [("tcol", 0, 16)])
     do("g", lambda q: q.iota(T.pix[:], [[0, 20]], 0, 1), [], [("pix", 0, 20)])
     do("g", lambda q: q.iota(T.uli[:], [[16, 8]], 0, 0), [], [("uli", 0, 8)])
-    do("g", lambda q: q.affine_select(T.et[:], T.eo[:], [[-1, 528]], op.is_equal, 0.0, 3, 4), [("eo", 0, 528)], [("et", 0, 528)])
     do("g", lambda q: q.iota(T.ident[:], [[1, H]], 0, 0, allow_small_or_imprecise_dtypes=True), [], [("ident", 0, H)])
+    do("g", lambda q: q.affine_select(T.et[:], T.eo[:], [[-1, 528]], op.is_equal, 0.0, 3, 4), [("eo", 0, 528)], [("et", 0, 528)])
     first = T.cores[rank ^ STEP[0]]
     lanes = topo.engines(core, first)
-    arrival([("mlp", 0, 20)], "arrm", len(lanes))
-    arrival([("msp", 0, 40)], "arrl0", len(lanes))
-    send(first, lanes, [(T.mli[:], T.mlp[:], ("mli", 0, 20))], "arrm")
+    if AHEAD:
+        arrival([("mlp", 0, 20)], "arrm", len(lanes))
+        send(first, lanes, [(T.mli[:], T.mlp[:], ("mli", 0, 20))], "arrm")
     ts(T.tm[:], T.tcol[:], 15, None, op.bitwise_and, None, [("tcol", 0, 16)], [("tm", 0, 16)])
     ts(T.qi[:], T.pix[:], 15, None, op.bitwise_and, None, [("pix", 0, 20)], [("qi", 0, 20)])
     ts(T.d2[:], T.tm[:], 0.0, -1.0, op.is_equal, op.mult, [("tm", 0, 16)], [("d2", 0, 16)])
@@ -226,11 +235,10 @@ def rank_program(g, core, T, topo):
     ts(T.qf[:], cols("qi", 0, 1), 14.5, 4.0, op.is_lt, op.mult, [("qi", 0, 1)], [("qf", 0, 1)])
     vcopy(T.ul[:], T.uli[:], [("uli", 0, 8)], [("ul", 0, 8)])
     ts(T.es[:], T.ds[:], 0.25, -8.0, op.min, op.mult, [("ds", 0, 16)], [("es", 0, 16)])
-    ts(col(BB), T.qf[:], -1.0, None, op.add, None, [("qf", 0, 1)], [("col", BB, BB + 1)])
-    scopy(cols("e0", 0, C - 16 * TWIST), T.es[:].indirect(T.qo[:, TWIST:20]), [("es", 0, 16), ("qo", 0, 20)], [("e0", 0, C)])
     line(T.d0[:], T.ds[:].indirect(T.qo[:, 0:20]), 1.0, 1.0, [("ds", 0, 16), ("qo", 0, 20)], [("d0", 0, C)])
-    for k, scale in ((S_OWN, 1.0 / (OWN[1] * UNIT)), (S_CUT, -2.0), (S_FAR, 1.0 / (FAR[1] * UNIT))):
-        scopy(col(k), col(INV), [("col", INV, INV + 1)], [("col", k, k + 1)], scale)
+    scopy(T.e0[:], T.es[:].indirect(T.qo[:, 0:10]), [("es", 0, 16), ("qo", 0, 20)], [("e0", 0, H)])
+    for k, scale, bias in ((C1, -1.0, 1.0), (CB, 0.5, -LIFT), (BM, 0.5, -1.0), (BN, -0.5, 0.0)):
+        line(col(k), T.qf[:], scale, bias, [("qf", 0, 1)], [("col", k, k + 1)])
 
     def table(q, out, region, code):
         if q == "v": ts(out, T.ident[:], float(code[1]), float(code[0]), op.mult, op.add, [("ident", 0, H)], [region])
@@ -265,31 +273,40 @@ def rank_program(g, core, T, topo):
     def places(m, out):
         return [lambda: ts(T.wk[:], T[m][:], H - 0.5, -float(H), op.is_gt, op.mult, [(m, 0, 20)], [("wk", 0, 20)]),
                 lambda: tt(T.kf[:], T[m][:], T.wk[:], op.add, [(m, 0, 20), ("wk", 0, 20)], [("kf", 0, 20)]),
-                lambda: (ts(cols(out, 0, 20), T.kf[:], 1.0 / UNIT, None, op.mult, None, [("kf", 0, 20)], [(out, 0, 20)]),
-                         ts(cols(out, 20, 40), T.kf[:], 1.0 / UNIT, col(BB), op.mult, op.add, [("kf", 0, 20), ("col", BB, BB + 1)], [(out, 20, 40)]))]
+                lambda: ts(T[out][:], T.kf[:], 1.0 / UNIT, LIFT, op.mult, op.add, [("kf", 0, 20)], [(out, 0, 20)])]
 
-    swaps, halves = T.sc[:, 15:C:16], T.sc[:, C + 15:2 * C:16]
+    def apart(kb, out):
+        tt(T[out][:], cols(kb, 0, 10), cols(kb, 10, 20), op.subtract, [(kb, 0, 20)], [(out, 0, 10)])
 
-    def swapped(out, src, region):
-        for k, o in ((0, op.subtract), (20, op.add)):
-            tt(cols(out, k, k + 20), src(k), swaps, o, [region(k), ("sc", 0, C)], [(out, k, k + 20)])
+    def lower_places():
+        for k, c in ((0, BM), (10, BN)):
+            line(cols("yy", k, k + 10), cols("kb", 10, 20), 1.0, col(c), [("kb", 10, 20), ("col", c, c + 1)], [("yy", k, k + 10)])
 
-    def offers():
-        for k in (0, 20):
-            tt(cols("pq", k, k + 20), halves, cols("kc", k, k + 20), op.add, [("sc", C, 2 * C), ("kc", k, k + 20)], [("pq", k, k + 20)])
+    def lane(name, w, k):
+        return T[name][:, 30 * w + k:30 * w + 30:3], (name, 30 * w, 30 * w + 30, k)
 
-    def larger():
-        for k in (0, 10):
-            tt(cols("nf", k, k + 10), cols("pq", k, k + 10), cols("pq", 30 - k, 40 - k), op.max, [("pq", 0, 40)], [("nf", k, k + 10)])
+    def entry(k):
+        return T.sc[:, 45 + 16 * k:480 + 16 * k:48], ("sc", 0, 512, k)
 
-    def addresses(out):
-        ts(T[out][:], T.nf[:], float(UNIT), None, op.mult, None, [("nf", 0, 20)], [(out, 0, 20)])
+    def add(out, w, k, in0, reg0, in1, reg1, plus):
+        view, region = lane(out, w, k)
+        tt(view, in0, in1, op.add if plus else op.subtract, [reg0, reg1], [region])
 
+    def choose(out, steps, a, n, src, region):
+        do("v", lambda q: q.tensor_tensor_scan(cols(out, a, a + n), cols(steps, a, a + n), src, 0.0, op.add, op.max), [(steps, a, a + n), region], [(out, a, a + n)])
+
+    def addresses(out, src, a, n, less):
+        ts(cols(out, a, a + n), T[src][:, 3 * a + 2:3 * (a + n):3], less, float(UNIT), op.add, op.mult, [(src, 3 * a, 3 * (a + n)), ("col", CB, CB + 1)], [(out, a, a + n)])
+
+    for name in ("dd", "pd", "msg") if AHEAD else ("dd",):
+        do("v", lambda q: q.memset(T[name][:], -100.0), [], [(name, 0, 60)])
     steps = places("mli", "kb")
-    unit(0)
-    unit(1)
+    table("v", cols("tab", 0, H), ("tab", 0, H), (1, 1))
+    table("v", cols("tab", TOP, WIN), ("tab", TOP, WIN), OWN)
+    table("v", *spots("wb", FAR), FAR)
     quant("uq", "uqs", "ut", 0, 128)
-    unit(2)
+    table("v", *spots("wb", OWN), OWN)
+    ts(col(CN), T.qf[:], -1.0, None, op.add, None, [("qf", 0, 1)], [("col", CN, CN + 1)])
     do("v", lambda q: q.tensor_copy(T.u2[:, 0:128].bitcast(dt.uint32), T.uq[:, 0:128].bitcast(dt.uint32).indirect(T.ul[:, 0:8])),
        [("uq", 0, 128), ("ul", 0, 8)], [("u2", 0, 128)])
     scopy(T.u2s[:, 0:128], T.uqs[:, 0:128].indirect(T.ul[:, 0:8]), [("uqs", 0, 128), ("ul", 0, 8)], [("u2s", 0, 128)])
@@ -299,15 +316,18 @@ def rank_program(g, core, T, topo):
     vcopy(T.mm[:], T.mli[:], [("mli", 0, 20)], [("mm", 0, 20)])
     plane("x0", 0, LO)
     scores_low_out()
+    unit(0)
     steps[1]()
     state_quant("x0", P2)
     scores(P2)
     steps[2]()
+    unit(1)
+    apart("kb", "dk")
     compare(0, P1)
-    for b in range(1, 4):
+    plane("x0", 1, LO)
+    lower_places()
+    for b in range(2, 4):
         plane("x0", b, LO)
-    table("s", cols("tab", 0, H), ("tab", 0, H), (1, 1))
-    table("s", cols("tab", TOP, WIN), ("tab", TOP, WIN), OWN)
 
     for r in range(3):
         last = r == 2
@@ -316,40 +336,49 @@ def rank_program(g, core, T, topo):
         ql, qls, pl, pls = "ql%d" % r, "qls%d" % r, "pl%d" % r, "pls%d" % r
         partner = T.cores[rank ^ STEP[r]]
         engines = topo.engines(core, partner)
-        if r: arrival([(npl, 0, 20)], "arrl%d" % r, len(engines))
+        ahead = AHEAD and r == 0
+        arrival([(npl, 0, 10)], "arrl%d" % r, len(engines))
+        arrival([("msp", 0, 30) if ahead else (npl, 10, 20)], "arrs%d" % r, len(engines))
         arrival([(pl, 0, H), (pls, 0, H)], "arrc%d" % r, 2 * len(engines))
 
         mates = "zo" if r else "mm"
         compare(r, P2)
-        pick("s", "gs", 16 * TWIST, "sw", CODES, mates, TWIST, 20 - TWIST, 0.25)
+        pick("s", "gs", H, "sw", CODES, mates, 10, 10, 0.25)
+        pick("s", "gs", 16 * TWIST, "sw", CODES, mates, TWIST, 10 - TWIST, 0.25)
         if r == 0:
             for b in range(4):
                 plane("x0", b, UP)
-        for a in (0, H):
-            scan_bits(a, H, *spots("sw", FAR if r else (H + 1, 1)))
+            for code in (OWN, FAR):
+                table("s", *spots("wa", code), code)
+        scan_bits(2, *spots("sw", FAR if r else (H + 1, 1)))
         pick("v", "gs", 0, "sw", CODES, mates, 0, TWIST, 0.25)
-        swapped("kc", lambda k: cols("kb", k, k + 20), lambda k: ("kb", k, k + 20))
-        for a, e in ((0, 16 * TWIST), (16 * TWIST, C)):
-            scan_bits(C + a, e - a, cols("gs", a, e), ("gs", a, e))
+        ts(T.ee[:], entry(2)[0], -2.0, col(C1), op.mult, op.add, [entry(2)[1], ("col", C1, C1 + 1)], [("ee", 0, 10)])
+        for w in range(2):
+            add("dd", w, 2, cols("yy", 10 * w, 10 * w + 10), ("yy", 0, 20), *entry(2), w == 0)
+        add("dd", 0, 1, T.dk[:], ("dk", 0, 10), T.ee[:], ("ee", 0, 10), True)
+        scan_bits(1, cols("gs", H, C), ("gs", H, C))
+        scan_bits(0, cols("gs", 0, H), ("gs", 0, H))
+        add("dd", 1, 1, T.dk[:], ("dk", 0, 10), T.ee[:], ("ee", 0, 10), False)
         if r == 0: unit(3)
-        if r == 0:
-            swapped("msg", lambda k: halves, lambda k: ("sc", C, 2 * C))
-            send(partner, engines, [(T.msg[:], T.msp[:], ("msg", 0, 40))], "arrl0")
-        steps = places("mlp", "pkb") if r == 0 else [lambda: None] * 3
-        offers()
-        steps[0]()
-        larger()
-        steps[1]()
-        addresses(nl)
-        steps[2]()
-        if r: send(partner, engines, [(T[nl][:], T[npl][:], (nl, 0, 20))], "arrl%d" % r)
+        for w in range(2):
+            choose("rr", "dd", 30 * w, 30, T.sc[:, 45:512:16], ("sc", 0, 512))
+        if ahead:
+            steps = places("mlp", None)
+            add("msg", 0, 0, *entry(0), *entry(2), True)
+        for w in range(2):
+            addresses(nl, "rr", 10 * w, 10, col(CB))
+            if w == 0 or not ahead:
+                send(partner, engines, [(cols(nl, 10 * w, 10 * w + 10), cols(npl, 10 * w, 10 * w + 10), (nl, 10 * w, 10 * w + 10))], ("arrl%d", "arrs%d")[w] % r)
+        if ahead:
+            add("msg", 0, 1, *entry(1), *entry(2), False)
+            send(partner, engines, [(T.msg[:], T.msp[:], ("msg", 0, 30))], "arrs0")
+            steps[0]()
+        if r == 0: unit(2)
         pick("s", "gw", TOP, "tab", WIN, nl, 10)
         if r == 0:
             table("s", cols("gw", 0, H), ("gw", 0, H), FAR)
-            for w in ("wa", "wb"):
-                for code in (OWN, FAR):
-                    table("s", *spots(w, code), code)
-            table("s", cols("wb", TOP, WIN), ("wb", TOP, WIN), OWN)
+            for w in sorted({("wa", "wb")[len(plan[0]) % 2] for plan in (HOME, AWAY)}):
+                table("s", cols(w, TOP, WIN), (w, TOP, WIN), OWN)
 
         def total(half, b, c=0, d=10):
             xp = "xp%d" % b
@@ -377,27 +406,18 @@ def rank_program(g, core, T, topo):
         def unpacked(q, b, k, code):
             evacuate(q, *spots("b%d" % b, code), k + b)
 
-        for b in range(4):
-            if r == 0 and b == 3: tt(T.pq[:], T.msp[:], T.pkb[:], op.add, [("msp", 0, 40), ("pkb", 0, 40)], [("pq", 0, 40)])
-            total(LO, b)
-        away = CODES_FIRST and topo.chip(core) != topo.chip(partner)
-        if r == 0: larger()
-        total(UP, 0, 0, 4 if away else 10)
-        if r == 0: addresses(npl)
-        quant("qz", "qzs", "z", H, H, H)
-        layer(0, LO)
-        if away:
-            total(UP, 0, 4, 10)
-            total(UP, 1, 0, 4)
-            for b in range(4):
-                made("sv"[b % 2], b, 0, LO)
-            total(UP, 1, 4, 10)
-            low_codes()
-        else: total(UP, 1, 0, 4)
+        def their_steps():
+            for k, src, region, bias in ((2, cols("kf", 10, 20), ("kf", 10, 20), LIFT), (1, T.pk[:], ("pk", 0, 10), col(CN))):
+                view, out = lane("pd", 0, k)
+                line(view, src, 1.0 / UNIT, bias, [region, ("col", CN, CN + 1)], [out])
 
-        pick("s", "wa", 0, "gw", WIN, npl, 0)
-        pick("s", "su", 0, "gw", WIN, npl, 10)
-        if not away: made("s", 0, 0, LO)
+        theirs = [steps[1], lambda: apart("kf", "pk")] if ahead else []
+        later = [lambda: choose("pr", "pd", 0, 30, T.msp[:], ("msp", 0, 30)),
+                 lambda: ts(cols(npl, 10, 20), T.pr[:, 2:30:3], -LIFT, float(UNIT), op.add, op.mult, [("pr", 0, 30)], [(npl, 10, 20)])] if ahead else []
+
+        def lower_layer():
+            quant("qz", "qzs", "z", H, H, H)
+            layer(0, LO)
 
         def upper_layer():
             quant("qz", "qzs", "z", 0, H)
@@ -405,45 +425,59 @@ def rank_program(g, core, T, topo):
 
         def upper_codes():
             quant("qu", "qus", "a", 0, H)
-            unpack(4, "qu", "qus")
-            unpack(0, pl, pls)
+            away = topo.chip(core) != topo.chip(partner)
+            for far, b in sorted([(far, b) for far in (0, 1) for b in range(4)], key=lambda e: e if away else e[::-1]):
+                product(b if far else 4 + b, "eq", "eqs", 128 * b, *((pl, pls) if far else ("qu", "qus")), 0, H)
 
-        behind_scan = {0: lambda: total(UP, 1, 4, 10), 1: low_codes, 2: lambda: total(UP, 2, 4, 10), 3: lambda: total(UP, 3, 4, 10), 4: upper_layer}
-        behind_list = {0: lambda: [made("v", b, 0, LO) for b in range(1, 4)], 1: lambda: total(UP, 2, 0, 4), 2: lambda: total(UP, 3, 0, 4),
-                       3: lambda: scan("ssu", "su", H), 4: lambda: entries("stu", "ssu", H), 5: lambda: made("v", 1, 4, UP),
-                       6: lambda: made("v", 2, 4, UP), 7: upper_codes}
-        behind_pick = {5: lambda: made("s", 0, 4, UP), 6: lambda: made("s", 3, 4, UP)}
-        if away:
-            behind_scan = {0: lambda: total(UP, 2, 0, 4), 1: lambda: total(UP, 3, 4, 10), 2: upper_layer, 3: lambda: entries("stu", "ssu", H)}
-            behind_list = {0: lambda: (total(UP, 2, 4, 10), total(UP, 3, 0, 4)), 2: lambda: scan("ssu", "su", H),
-                           3: lambda: made("v", 0, 4, UP), 4: lambda: made("v", 2, 4, UP), 5: upper_codes}
-            behind_pick = {3: lambda: made("s", 1, 4, UP), 4: lambda: made("s", 3, 4, UP)}
+        def fill(calls):
+            for c in calls.split():
+                if c[0] == "z": total(UP, int(c[1]), *{"": (0, 10), "a": (0, 4), "b": (4, 10)}[c[2:]])
+                elif c[0] == "y": total(LO, int(c[1]))
+                elif c[0] == "l": made(c[2], int(c[1]), 0, LO)
+                elif c[0] == "u": made(c[2], int(c[1]), 4, UP)
+                elif c[0] == "o": unpacked(c[2], int(c[1]), 4, OWN)
+                elif c[0] == "f": unpacked(c[2], int(c[1]), 0, FAR)
+                elif c[0] == "p": pick(c[1], "su", 0, "gw", WIN, npl, 10)
+                else: {"Y": lower_layer, "A": low_codes, "Z": upper_layer, "B": upper_codes, "S": lambda: scan("ssu", "su", H), "E": lambda: entries("stu", "ssu", H)}[c]()
+
+        JUMPS, FILL = AWAY if topo.chip(core) != topo.chip(partner) else HOME
+        for c in FILL["sums"].split():
+            fill(c)
+            if theirs: theirs.pop(0)()
+        while theirs: theirs.pop(0)()
+
+        pick("s", "wa", 0, "gw", WIN, npl, 0)
+        if ahead: their_steps()
+        if HALF: pick("s", "gw", TOP, "wa", WIN, nl, 10)
+        fill(FILL["first"])
         win, nxt, power, lists = "wa", "wb", 1, {}
-        for k, (by, share) in enumerate(JUMPS):
+        for k, (by, share, behind_pick, behind_scan, behind_list) in enumerate(JUMPS):
             def step(q, c, d): pick(q, nxt, 16 * c, win, CODES, lists[by], c, d - c)
-            fresh = power in [j for j, _ in JUMPS]
+            fresh = power in [j[0] for j in JUMPS]
             if k: step("s", share, 10)
-            if k in behind_pick: behind_pick[k]()
-            scn, lu = "scn%d" % (k % 3), "lu%d" % (k % 3)
+            elif HALF: pick("s", nxt, 0, "gw", WIN, npl, 0)
+            fill(behind_pick)
+            scn, lu = "scn%d" % (k % 4), "lu%d" % (k % 4)
             if fresh: scan(scn, win, H)
-            if share: step("v", 0, share)
-            if k in behind_scan: behind_scan[k]()
+            if share and k: step("v", 0, share)
+            fill(behind_scan)
             if fresh:
                 entries(lu, scn, H)
                 lists[power] = lu
-            if k == 0: step("s", 0, 10)
-            if k in behind_list: behind_list[k]()
+            if k == 0 and not HALF:
+                step("s", share, 10)
+                if share: step("v", 0, share)
+            if later: later.pop(0)()
+            fill(behind_list)
             win, nxt, power = nxt, win, power + by
-        if r == 0: quant("vq", "vqs", "vt", 0, 128)
         pick("v", "cf", 0, win, WIN, nl, 0)
         pick("s", "cf", H, win, CODES, "stu", 0)
-        unpacked("v", 0, 4, OWN)
+        fill(FILL["ends"])
         scan("csc", "cf", C)
-        unpacked("v", 1, 4, OWN)
+        if r == 1: quant("vq", "vqs", "vt", 0, 128)
+        fill(FILL["scan"])
         entries("zo", "csc", C)
-        for b in range(4):
-            if b > 1: unpacked("s", b, 4, OWN)
-            unpacked("s", b, 0, FAR)
+        fill(FILL["list"])
 
         def renew(part, b):
             bb = "b%d" % b
@@ -451,8 +485,11 @@ def rank_program(g, core, T, topo):
             tt(T[xn][:, 4 * lo + b:4 * hi:4], T[bb][:, 0:CODES].indirect(T.zo[:, lo // 16:hi // 16]), T[x][:, 4 * lo + b:4 * hi:4], op.add,
                [(bb, 0, CODES), ("zo", lo // 16, hi // 16), (x, lo, hi, b)], [(xn, lo, hi, b)])
 
+        if r == 0:
+            for k, scale in ((S_OWN, 1.0 / (OWN[1] * UNIT)), (S_CUT, -16.0), (S_FAR, 1.0 / (FAR[1] * UNIT))):
+                scopy(col(k), col(INV), [("col", INV, INV + 1)], [("col", k, k + 1)], scale)
         if not last:
-            for k, (s, b) in enumerate(((S_OWN, -OWN[0] / (OWN[1] * UNIT)), (S_CUT, 2.0 * (FAR[0] - 6)), (S_FAR, -FAR[0] / (FAR[1] * UNIT)))):
+            for k, (s, b) in enumerate(((S_OWN, LIFT - OWN[0] / (OWN[1] * UNIT)), (S_CUT, 16.0 * (FAR[0] - 6)), (S_FAR, LIFT - FAR[0] / (FAR[1] * UNIT)))):
                 line(cols("ka", 20 * k, 20 * k + 20), T.csc[:, 15:C:16], col(s), b, [("csc", 0, C), ("col", s, s + 1)], [("ka", 20 * k, 20 * k + 20)])
         else:
             for code, first_column in ((OWN, 0.0), (FAR, float(H))):
@@ -460,26 +497,27 @@ def rank_program(g, core, T, topo):
                 line(view, T.ident[:], 1.0, first_column, [("ident", 0, H)], [region])
             pick("s", "mof", 0, "fin", CODES, "zo", 0, 20)
         for b in range(4):
-            renew(P1 if b else (0, C), b)
+            renew(P1 if b >= WHOLE else (0, C), b)
             if not last: plane(xn, b, LO)
-        renew(P2, 1)
+        renew(P2, WHOLE)
         state_quant(xn, P1)
         if not last:
             scores(P1)
             scores_low_out()
         else: scores(P1, "vq", "vqs")
-        for b in range(2, 4):
+        for b in range(WHOLE + 1, 4):
             renew(P2, b)
         if not last:
             tt(T.kf[:], cols("ka", 0, 20), cols("ka", 20, 40), op.min, [("ka", 0, 40)], [("kf", 0, 20)])
         state_quant(xn, P2)
         if not last:
             scores(P2)
-            tt(cols("kb", 0, 20), T.kf[:], cols("ka", 40, 60), op.max, [("kf", 0, 20), ("ka", 40, 60)], [("kb", 0, 20)])
+            tt(T.kb[:], T.kf[:], cols("ka", 40, 60), op.max, [("kf", 0, 20), ("ka", 40, 60)], [("kb", 0, 20)])
             compare(r + 1, P1)
-            ts(cols("kb", 20, 40), cols("kb", 0, 20), col(BB), None, op.add, None, [("kb", 0, 20), ("col", BB, BB + 1)], [("kb", 20, 40)])
+            apart("kb", "dk")
             for b in range(4):
                 plane(xn, b, UP)
+                if b == 1: lower_places()
         else: scores(P2, "vq", "vqs")
 
     def store(q, out, in_, region):

from concourse.mybir import dt, AluOpType, ActivationFunctionType

BF, F32, I32, U16, U8, MX = "bfloat16", "float32", "int32", "uint16", "uint8", "float8_e4m3fn_x4"
STEP = [1, 2, 4]
C, H = 320, 160
TOP = 2048
WIN = TOP + H
OWN, FAR = (162, 2), (488, 8)
CODES = FAR[0] + FAR[1] * H

SCRATCH = {
    "x0": ("sbuf", [128, 4 * C], BF), "x1": ("sbuf", [128, 4 * C], BF), "x2": ("sbuf", [128, 4 * C], BF), "x3": ("sbuf", [128, 4 * C], BF),
    "z": ("sbuf", [128, 4 * C], BF), "a": ("sbuf", [128, 4 * C], BF),
    "et": ("sbuf", [128, 528], BF), "eo": ("sbuf", [128, 528], BF), "eq": ("sbuf", [128, 512], MX), "eqs": ("sbuf", [128, 512], U8),
    "ut": ("sbuf", [128, 512], BF), "uq": ("sbuf", [128, 128], MX), "uqs": ("sbuf", [128, 128], U8),
    "u2": ("sbuf", [128, 128], MX), "u2s": ("sbuf", [128, 128], U8),
    "vt": ("sbuf", [128, 512], BF), "vq": ("sbuf", [128, 128], MX), "vqs": ("sbuf", [128, 128], U8),
    "wq": ("sbuf", [128, 512], MX), "wqs": ("sbuf", [128, 512], U8),
    "qx": ("sbuf", [128, C], MX), "qxs": ("sbuf", [128, C], U8),
    "qz": ("sbuf", [128, C], MX), "qzs": ("sbuf", [128, C], U8),
    "qu": ("sbuf", [128, H], MX), "qus": ("sbuf", [128, H], U8),
    "ps": ("psum", [128, 4096], F32),
    "slo": ("sbuf", [128, H], F32), "sw": ("sbuf", [128, CODES], BF), "gs": ("sbuf", [128, C], BF), "sc": ("sbuf", [128, 512], BF),
    "mli": ("sbuf", [128, 20], I32), "wk": ("sbuf", [128, 20], F32), "kf": ("sbuf", [128, 20], F32),
    "kb": ("sbuf", [128, 20], F32), "mm": ("sbuf", [128, 20], U16), "ka": ("sbuf", [128, 60], F32), "dk": ("sbuf", [128, 10], F32),
    "yy": ("sbuf", [128, 20], F32), "ee": ("sbuf", [128, 10], F32), "dd": ("sbuf", [128, 60], F32), "rr": ("sbuf", [128, 60], F32),
    "mlp": ("sbuf", [128, 20], I32), "pkb": ("sbuf", [128, 20], F32), "pk": ("sbuf", [128, 10], F32), "pd": ("sbuf", [128, 30], F32),
    "pr": ("sbuf", [128, 30], F32), "msg": ("sbuf", [128, 30], BF), "msp": ("sbuf", [128, 30], BF),
    "ident": ("sbuf", [128, H], BF), "tab": ("sbuf", [128, WIN], BF), "gw": ("sbuf", [128, WIN], BF),
    "wa": ("sbuf", [128, WIN], BF), "wb": ("sbuf", [128, WIN], BF),
    "su": ("sbuf", [128, H], BF), "ssu": ("sbuf", [128, H], BF), "stu": ("sbuf", [128, 10], U16),
    "cf": ("sbuf", [128, C], BF), "csc": ("sbuf", [128, C], BF), "zo": ("sbuf", [128, 20], U16),
    "fin": ("sbuf", [128, CODES], F32), "mof": ("sbuf", [128, C], F32), "yb": ("sbuf", [128, C], F32),
    "d0": ("sbuf", [128, C], BF), "ds": ("sbuf", [128, 16], F32), "d1": ("sbuf", [128, 16], F32), "d2": ("sbuf", [128, 16], F32), "tcol": ("sbuf", [128, 16], I32),
    "pix": ("sbuf", [128, 20], I32), "qi": ("sbuf", [128, 20], I32), "qo": ("sbuf", [128, 20], U16), "qf": ("sbuf", [128, 1], F32), "tm": ("sbuf", [128, 16], I32),
    "e0": ("sbuf", [128, H], BF), "es": ("sbuf", [128, 16], F32), "col": ("sbuf", [128, 10], F32),
    "uli": ("sbuf", [128, 8], I32), "ul": ("sbuf", [128, 8], U16),
}
for _b in range(4):
    SCRATCH["xp%d" % _b] = ("sbuf", [128, WIN], BF)
    SCRATCH["b%d" % _b] = ("sbuf", [128, CODES], BF)
    SCRATCH["scn%d" % _b] = ("sbuf", [128, H], BF)
    SCRATCH["lu%d" % _b] = ("sbuf", [128, 10], U16)
for _r in range(3):
    SCRATCH["nl%d" % _r] = ("sbuf", [128, 20], U16)
    SCRATCH["np%d" % _r] = ("sbuf", [128, 20], U16)
    SCRATCH["ql%d" % _r] = ("sbuf", [128, H], MX)
    SCRATCH["qls%d" % _r] = ("sbuf", [128, H], U8)
    SCRATCH["pl%d" % _r] = ("sbuf", [128, H], MX)
    SCRATCH["pls%d" % _r] = ("sbuf", [128, H], U8)
SEMAPHORES = ["sv", "ss", "st", "sg", "sent", "outs", "ldxl", "ldxu", "ldu", "ldm", "ldw", "ldws", "ldv", "arrm"]
for _r in range(3):
    SEMAPHORES += ["arrl%d" % _r, "arrs%d" % _r, "arrc%d" % _r]

LO, UP = (H, C), (0, H)
CUT = 128
P1, P2 = (CUT, C), (0, CUT)
HOME = ([(1, 0, "l0s", "z1b", "l2s z3a z2 l1v"), (1, 0, "l3s", "z3b", ""), (2, 0, "ps", "Z A", ""), (3, 4, "u0s", "", "S"), (5, 4, "u1s", "", "E"),
         (8, 4, "u2s", "", "u3v"), (13, 4, "", "", "B"), (13, 4, "", "", ""), (34, 6, "", "", "")],
        {"sums": "y0 y1 y2 y3 z0 Y z1a", "first": "", "ends": "o0s", "scan": "", "list": "f0s o1v o2s f1s f2s f3s o3s"})
AWAY = ([(1, 0, "l1s l3s l2v", "z3b", "A z2 z3a"), (1, 0, "ps", "Z", ""), (2, 6, "", "", "S"), (3, 4, "u1s", "", "E"), (5, 6, "u0s", "", ""),
         (8, 4, "u2s", "", "u3v"), (13, 4, "", "", ""), (13, 2, "B", "", ""), (34, 6, "", "o0v", "")],
        {"sums": "y0 y1 y2 y3 z1a Y z0 z1b l0v", "first": "", "ends": "o1s", "scan": "", "list": "o2s f0s f1s f2s f3s o3s"})
HALF = False
AHEAD = True
WHOLE = 1
TWIST = 6
UNIT, LIFT = 4 * TOP, 8.0
INV, S_OWN, S_CUT, S_FAR, C1, CB, BM, BN, CL, CN = range(10)


def rank_program(g, core, T, topo):
    rank = T.rank_of(core)
    if rank is None:
        return
    queues = {"v": g.vector, "s": g.scalar, "t": g.tensor, "g": g, "y": g.sync}
    home = {"v": "sv", "s": "ss", "t": "st", "g": "sg"}
    count = {}
    known = {q: {} for q in queues}
    snap = {}
    log = {}

    def meets(e, r):
        return e[0] < r[2] and r[1] < e[1] and (e[2] is None or r[3] is None or e[2] == r[3])

    def full(r):
        return (r[0], r[1], r[2], r[3] if len(r) > 3 else None)

    def hold(q, need):
        while need:
            best = None
            for s, v in sorted(need):
                covers = sum(1 for s2, v2 in need if snap[(s, v)].get(s2, 0) >= v2)
                if best is None or covers > best[0]: best = (covers, s, v)
            _, s, v = best
            queues[q].wait_ge(T.sem[s], v)
            for s2, v2 in snap[(s, v)].items():
                if known[q].get(s2, 0) < v2: known[q][s2] = v2
            need = [(s2, v2) for s2, v2 in need if known[q].get(s2, 0) < v2]

    def waits(q, reads, writes):
        need = set()
        for r in reads:
            for e in log.get(r[0], []):
                if e[6] and meets(e, r): need.add((e[3], e[4]))
        for r in writes:
            for e in log.get(r[0], []):
                if meets(e, r): need.add((e[3], e[4]))
        hold(q, [(s, v) for s, v in need if known[q].get(s, 0) < v])

    def record(q, reads, writes, s, v):
        for r in writes:
            log[r[0]] = [e for e in log.get(r[0], []) if not (r[1] <= e[0] and e[1] <= r[2] and (r[3] is None or r[3] == e[2]))]
            log[r[0]].append((r[1], r[2], r[3], s, v, q, True))
        for r in reads:
            log.setdefault(r[0], []).append((r[1], r[2], r[3], s, v, q, False))

    def do(q, call, reads, writes, sem=None):
        reads, writes = [full(r) for r in reads], [full(r) for r in writes]
        waits(q, reads, writes)
        inc = 16 if sem else 1
        s = sem or home[q]
        call(queues[q]).then_inc(T.sem[s], inc)
        count[s] = count.get(s, 0) + inc
        snap[(s, count[s])] = dict(known[q])
        snap[(s, count[s])][s] = count[s]
        record(q, reads, writes, s, count[s])

    def send(dst, engines, pairs, sem):
        rid, pid, _ = topo.addr(dst)
        m = sum(1 << e for e in engines)
        for src, land, region in pairs:
            waits("g", [full(region)], [])
            g.remote_dma(land, src, T.sem[sem], T.sem.sent, pid, rid, m)
            count["sent"] = count.get("sent", 0) + len(engines)

    def arrival(regions, sem, n):
        count[sem] = n
        snap[(sem, n)] = {sem: n}
        record("remote", [], [full(r) for r in regions], sem, n)

    op = AluOpType
    COPY, SAME = ActivationFunctionType.Copy, ActivationFunctionType.Identity

    def cols(name, a, b):
        return T[name][:, a:b]

    def col(k):
        return T.col[:, k:k + 1]

    def spots(name, code):
        a, e = code[0] - 1, code[0] - 1 + code[1] * H
        return T[name][:, a:e:code[1]], (name, a, e)

    def tt(out, in0, in1, o, reads, writes):
        do("v", lambda q: q.tensor_tensor(out, in0, in1, o), reads, writes)

    def ts(out, in0, s1, s2, o1, o2, reads, writes):
        if o2 is None:
            do("v", lambda q: q.tensor_scalar(out, in0, s1, None, o1), reads, writes)
        else:
            do("v", lambda q: q.tensor_scalar(out, in0, s1, s2, o1, o2), reads, writes)

    def vcopy(out, in_, reads, writes):
        do("v", lambda q: q.tensor_copy(out, in_), reads, writes)

    def scopy(out, in_, reads, writes, scale=1.0):
        if scale == 1.0: do("s", lambda q: q.activation(out, in_, COPY), reads, writes)
        else: do("s", lambda q: q.activation(out, in_, COPY, scale=scale), reads, writes)

    def line(out, in_, scale, bias, reads, writes):
        do("s", lambda q: q.activation(out, in_, SAME, bias=bias, scale=scale), reads, writes)

    def pick(q, name, o, win, wn, off, a, n=10, scale=1.0):
        out, in_, reads, writes = cols(name, o, o + 16 * n), T[win][:, 0:wn].indirect(T[off][:, a:a + n]), [(win, 0, wn), (off, a, a + n)], [(name, o, o + 16 * n)]
        if q == "s": scopy(out, in_, reads, writes, scale)
        elif scale == 1.0: vcopy(out, in_, reads, writes)
        else: ts(out, in_, scale, None, op.mult, None, reads, writes)

    def scan(out, src, n):
        do("v", lambda q: q.tensor_tensor_scan(cols(out, 0, n), cols("d0", 0, n), cols(src, 0, n), 0.0, op.mult, op.max), [("d0", 0, C), (src, 0, n)], [(out, 0, n)])

    def scan_bits(k, src, region):
        do("v", lambda q: q.tensor_tensor_scan(T.sc[:, 16 * k:16 * k + 3 * H:3], T.e0[:], src, 0.0, op.add, op.min), [("e0", 0, H), region], [("sc", 0, 512, k)])

    def entries(out, src, n):
        ts(cols(out, 0, n // 16), T[src][:, 15:n:16], col(INV), -1.0, op.mult, op.add, [(src, 0, n), ("col", INV, INV + 1)], [(out, 0, n // 16)])

    def quant(out, scales, tile, a, n, dst=0):
        do("v", lambda q: q.quantize_mx(T[out][:, dst:dst + n], T[scales][:, dst:dst + n], T[tile][:, 4 * a:4 * (a + n)]),
           [(tile, a, a + n)], [(out, dst, dst + n), (scales, dst, dst + n)])

    def psum(bank, n):
        return T.ps[:, 512 * bank:512 * bank + n]

    def product(bank, w, ws, wa, x, xs, a, n):
        do("t", lambda q: q.matmul_mx(psum(bank, n), T[w][:, wa:wa + 128], T[ws][:, wa:wa + 128], T[x][:, a:a + n], T[xs][:, a:a + n], True, True),
           [(w, wa, wa + 128), (ws, wa, wa + 128), (x, a, a + n), (xs, a, a + n)], [("bank%d" % bank, 0, 512)])

    def evacuate(q, out, oreg, bank, scale=1.0, a=0, n=H):
        src = T.ps[:, 512 * bank + a:512 * bank + a + n]
        if q == "s": scopy(out, src, [("bank%d" % bank, 0, 512)], [oreg], scale)
        else: ts(out, src, scale, None, op.mult, None, [("bank%d" % bank, 0, 512)], [oreg])

    def load(q, out, in_, region, sem):
        do(q, lambda e: e.dma_start(out, in_), [], [region], sem)

    load("s", T.ut[:], T.u[:], ("ut", 0, 128), "ldu")
    load("s", T.mli[:], T.ml[:], ("mli", 0, 20), "ldm")
    load("y", cols("x0", 4 * CUT, 4 * C), T.x[:, 4 * CUT:4 * C], ("x0", CUT, C), "ldxl")
    load("y", cols("x0", 0, 4 * CUT), T.x[:, 0:4 * CUT], ("x0", 0, CUT), "ldxu")
    waits("y", [full(("x0", 0, C))], [])
    load("y", T.wq[:].bitcast(dt.uint8), T.wc[:], ("wq", 0, 512), "ldw")
    load("y", T.wqs[:], T.ws[:], ("wqs", 0, 512), "ldws")
    load("y", T.vt[:], T.v[:], ("vt", 0, 128), "ldv")

    do("v", lambda q: q.memset(T.eo[:], 1.0), [], [("eo", 0, 528)])
    do("g", lambda q: q.iota(T.tcol[:], [[1, 16]], 128, -1), [], [("tcol", 0, 16)])
    do("g", lambda q: q.iota(T.pix[:], [[0, 20]], 0, 1), [], [("pix", 0, 20)])
    do("g", lambda q: q.iota(T.uli[:], [[16, 8]], 0, 0), [], [("uli", 0, 8)])
    do("g", lambda q: q.iota(T.ident[:], [[1, H]], 0, 0, allow_small_or_imprecise_dtypes=True), [], [("ident", 0, H)])
    do("g", lambda q: q.affine_select(T.et[:], T.eo[:], [[-1, 528]], op.is_equal, 0.0, 3, 4), [("eo", 0, 528)], [("et", 0, 528)])
    first = T.cores[rank ^ STEP[0]]
    lanes = topo.engines(core, first)
    if AHEAD:
        arrival([("mlp", 0, 20)], "arrm", len(lanes))
        send(first, lanes, [(T.mli[:], T.mlp[:], ("mli", 0, 20))], "arrm")
    ts(T.tm[:], T.tcol[:], 15, None, op.bitwise_and, None, [("tcol", 0, 16)], [("tm", 0, 16)])
    ts(T.qi[:], T.pix[:], 15, None, op.bitwise_and, None, [("pix", 0, 20)], [("qi", 0, 20)])
    ts(T.d2[:], T.tm[:], 0.0, -1.0, op.is_equal, op.mult, [("tm", 0, 16)], [("d2", 0, 16)])
    ts(T.d1[:], T.tm[:], 1.0, TOP - 1.0, op.is_equal, op.mult, [("tm", 0, 16)], [("d1", 0, 16)])
    vcopy(T.qo[:], T.qi[:], [("qi", 0, 20)], [("qo", 0, 20)])
    ts(col(INV), cols("qi", 0, 1), 14.5, 1.0 / TOP, op.is_gt, op.max, [("qi", 0, 1)], [("col", INV, INV + 1)])
    tt(T.ds[:], T.d2[:], T.d1[:], op.add, [("d2", 0, 16), ("d1", 0, 16)], [("ds", 0, 16)])
    ts(T.qf[:], cols("qi", 0, 1), 14.5, 4.0, op.is_lt, op.mult, [("qi", 0, 1)], [("qf", 0, 1)])
    vcopy(T.ul[:], T.uli[:], [("uli", 0, 8)], [("ul", 0, 8)])
    ts(T.es[:], T.ds[:], 0.25, -8.0, op.min, op.mult, [("ds", 0, 16)], [("es", 0, 16)])
    line(T.d0[:], T.ds[:].indirect(T.qo[:, 0:20]), 1.0, 1.0, [("ds", 0, 16), ("qo", 0, 20)], [("d0", 0, C)])
    scopy(T.e0[:], T.es[:].indirect(T.qo[:, 0:10]), [("es", 0, 16), ("qo", 0, 20)], [("e0", 0, H)])
    for k, scale, bias in ((C1, -1.0, 1.0), (CB, 0.5, -LIFT), (BM, 0.5, -1.0), (BN, -0.5, 0.0)):
        line(col(k), T.qf[:], scale, bias, [("qf", 0, 1)], [("col", k, k + 1)])

    def table(q, out, region, code):
        if q == "v": ts(out, T.ident[:], float(code[1]), float(code[0]), op.mult, op.add, [("ident", 0, H)], [region])
        else: line(out, T.ident[:], float(code[1]), float(code[0]), [("ident", 0, H)], [region])

    def unit(b):
        do("v", lambda q: q.quantize_mx(cols("eq", 128 * b, 128 * b + 128), cols("eqs", 128 * b, 128 * b + 128), cols("et", 3 - b, 515 - b)),
           [("et", 0, 528)], [("eq", 128 * b, 128 * b + 128), ("eqs", 128 * b, 128 * b + 128)])

    def scores(part, w="u2", ws="u2s"):
        product(0 if part == P1 else 4, w, ws, 0, "qx", "qxs", part[0], part[1] - part[0])

    def state_quant(x, part):
        quant("qx", "qxs", x, part[0], part[1] - part[0], part[0])

    def compare(r, part):
        a, e, bank, at = (CUT, H, 0, 0) if part == P1 else (0, CUT, 4, 0)
        for code, o in ((FAR if r else (H + 1, 1), op.is_gt), (OWN if r else (1, 1), op.is_le)):
            lo, hi = code[0] - 1 + code[1] * a, code[0] - 1 + code[1] * e
            tt(T.sw[:, lo:hi:code[1]], psum(bank, e - a), cols("slo", a, e), o, [("bank%d" % bank, 0, 512), ("slo", a, e)], [("sw", lo, hi)])

    def address(half):
        return (0, H) if half == LO else (TOP, WIN)

    def plane(x, b, half):
        a, e = address(half)
        scopy(cols("xp%d" % b, a, e), T[x][:, 4 * half[0] + b:4 * half[1]:4], [(x, half[0], half[1], b)], [("xp%d" % b, a, e)])

    def scores_low_out():
        evacuate("s", T.slo[:], ("slo", 0, H), 0, 1.0, H - CUT)

    def places(m, out):
        return [lambda: ts(T.wk[:], T[m][:], H - 0.5, -float(H), op.is_gt, op.mult, [(m, 0, 20)], [("wk", 0, 20)]),
                lambda: tt(T.kf[:], T[m][:], T.wk[:], op.add, [(m, 0, 20), ("wk", 0, 20)], [("kf", 0, 20)]),
                lambda: ts(T[out][:], T.kf[:], 1.0 / UNIT, LIFT, op.mult, op.add, [("kf", 0, 20)], [(out, 0, 20)])]

    def apart(kb, out):
        tt(T[out][:], cols(kb, 0, 10), cols(kb, 10, 20), op.subtract, [(kb, 0, 20)], [(out, 0, 10)])

    def lower_places():
        for k, c in ((0, BM), (10, BN)):
            line(cols("yy", k, k + 10), cols("kb", 10, 20), 1.0, col(c), [("kb", 10, 20), ("col", c, c + 1)], [("yy", k, k + 10)])

    def lane(name, w, k):
        return T[name][:, 30 * w + k:30 * w + 30:3], (name, 30 * w, 30 * w + 30, k)

    def entry(k):
        return T.sc[:, 45 + 16 * k:480 + 16 * k:48], ("sc", 0, 512, k)

    def add(out, w, k, in0, reg0, in1, reg1, plus):
        view, region = lane(out, w, k)
        tt(view, in0, in1, op.add if plus else op.subtract, [reg0, reg1], [region])

    def choose(out, steps, a, n, src, region):
        do("v", lambda q: q.tensor_tensor_scan(cols(out, a, a + n), cols(steps, a, a + n), src, 0.0, op.add, op.max), [(steps, a, a + n), region], [(out, a, a + n)])

    def addresses(out, src, a, n, less):
        ts(cols(out, a, a + n), T[src][:, 3 * a + 2:3 * (a + n):3], less, float(UNIT), op.add, op.mult, [(src, 3 * a, 3 * (a + n)), ("col", CB, CB + 1)], [(out, a, a + n)])

    for name in ("dd", "pd", "msg") if AHEAD else ("dd",):
        do("v", lambda q: q.memset(T[name][:], -100.0), [], [(name, 0, 60)])
    steps = places("mli", "kb")
    table("v", cols("tab", 0, H), ("tab", 0, H), (1, 1))
    table("v", cols("tab", TOP, WIN), ("tab", TOP, WIN), OWN)
    table("v", *spots("wb", FAR), FAR)
    quant("uq", "uqs", "ut", 0, 128)
    table("v", *spots("wb", OWN), OWN)
    ts(col(CN), T.qf[:], -1.0, None, op.add, None, [("qf", 0, 1)], [("col", CN, CN + 1)])
    do("v", lambda q: q.tensor_copy(T.u2[:, 0:128].bitcast(dt.uint32), T.uq[:, 0:128].bitcast(dt.uint32).indirect(T.ul[:, 0:8])),
       [("uq", 0, 128), ("ul", 0, 8)], [("u2", 0, 128)])
    scopy(T.u2s[:, 0:128], T.uqs[:, 0:128].indirect(T.ul[:, 0:8]), [("uqs", 0, 128), ("ul", 0, 8)], [("u2s", 0, 128)])
    state_quant("x0", P1)
    scores(P1)
    steps[0]()
    vcopy(T.mm[:], T.mli[:], [("mli", 0, 20)], [("mm", 0, 20)])
    plane("x0", 0, LO)
    scores_low_out()
    unit(0)
    steps[1]()
    state_quant("x0", P2)
    scores(P2)
    steps[2]()
    unit(1)
    apart("kb", "dk")
    compare(0, P1)
    plane("x0", 1, LO)
    lower_places()
    for b in range(2, 4):
        plane("x0", b, LO)

    for r in range(3):
        last = r == 2
        x, xn = "x%d" % r, "x%d" % (r + 1)
        nl, npl = "nl%d" % r, "np%d" % r
        ql, qls, pl, pls = "ql%d" % r, "qls%d" % r, "pl%d" % r, "pls%d" % r
        partner = T.cores[rank ^ STEP[r]]
        engines = topo.engines(core, partner)
        ahead = AHEAD and r == 0
        arrival([(npl, 0, 10)], "arrl%d" % r, len(engines))
        arrival([("msp", 0, 30) if ahead else (npl, 10, 20)], "arrs%d" % r, len(engines))
        arrival([(pl, 0, H), (pls, 0, H)], "arrc%d" % r, 2 * len(engines))

        mates = "zo" if r else "mm"
        compare(r, P2)
        pick("s", "gs", H, "sw", CODES, mates, 10, 10, 0.25)
        pick("s", "gs", 16 * TWIST, "sw", CODES, mates, TWIST, 10 - TWIST, 0.25)
        if r == 0:
            for b in range(4):
                plane("x0", b, UP)
            for code in (OWN, FAR):
                table("s", *spots("wa", code), code)
        scan_bits(2, *spots("sw", FAR if r else (H + 1, 1)))
        pick("v", "gs", 0, "sw", CODES, mates, 0, TWIST, 0.25)
        ts(T.ee[:], entry(2)[0], -2.0, col(C1), op.mult, op.add, [entry(2)[1], ("col", C1, C1 + 1)], [("ee", 0, 10)])
        for w in range(2):
            add("dd", w, 2, cols("yy", 10 * w, 10 * w + 10), ("yy", 0, 20), *entry(2), w == 0)
        add("dd", 0, 1, T.dk[:], ("dk", 0, 10), T.ee[:], ("ee", 0, 10), True)
        scan_bits(1, cols("gs", H, C), ("gs", H, C))
        scan_bits(0, cols("gs", 0, H), ("gs", 0, H))
        add("dd", 1, 1, T.dk[:], ("dk", 0, 10), T.ee[:], ("ee", 0, 10), False)
        if r == 0: unit(3)
        for w in range(2):
            choose("rr", "dd", 30 * w, 30, T.sc[:, 45:512:16], ("sc", 0, 512))
        if ahead:
            steps = places("mlp", None)
            add("msg", 0, 0, *entry(0), *entry(2), True)
        for w in range(2):
            addresses(nl, "rr", 10 * w, 10, col(CB))
            if w == 0 or not ahead:
                send(partner, engines, [(cols(nl, 10 * w, 10 * w + 10), cols(npl, 10 * w, 10 * w + 10), (nl, 10 * w, 10 * w + 10))], ("arrl%d", "arrs%d")[w] % r)
        if ahead:
            add("msg", 0, 1, *entry(1), *entry(2), False)
            send(partner, engines, [(T.msg[:], T.msp[:], ("msg", 0, 30))], "arrs0")
            steps[0]()
        if r == 0: unit(2)
        pick("s", "gw", TOP, "tab", WIN, nl, 10)
        if r == 0:
            table("s", cols("gw", 0, H), ("gw", 0, H), FAR)
            for w in sorted({("wa", "wb")[len(plan[0]) % 2] for plan in (HOME, AWAY)}):
                table("s", cols(w, TOP, WIN), (w, TOP, WIN), OWN)

        def total(half, b, c=0, d=10):
            xp = "xp%d" % b
            o = 10 if half == LO else 0
            lo, hi = half[0] + 16 * c, half[0] + 16 * d
            tt(T.z[:, 4 * lo + b:4 * hi:4], T[xp][:, 0:WIN].indirect(T[nl][:, o + c:o + d]), T[x][:, 4 * lo + b:4 * hi:4], op.add,
               [(xp, 0, WIN), (nl, o + c, o + d), (x, lo, hi, b)], [("z", lo, hi, b)])

        def layer(k, half):
            for b in range(4):
                product(k + b, "wq", "wqs", 128 * b, "qz", "qzs", half[0], H)

        def made(q, b, k, half):
            evacuate(q, T.a[:, 4 * half[0] + b:4 * half[1]:4], ("a", half[0], half[1], b), k + b, 0.015625)

        def low_codes():
            quant(ql, qls, "a", H, H)
            send(partner, engines, [(T[ql][:, 0:H].bitcast(dt.uint8), T[pl][:, 0:H].bitcast(dt.uint8), (ql, 0, H)),
                                    (T[qls][:, 0:H], T[pls][:, 0:H], (qls, 0, H))], "arrc%d" % r)

        def unpack(k, q, qs):
            for b in range(4):
                product(k + b, "eq", "eqs", 128 * b, q, qs, 0, H)

        def unpacked(q, b, k, code):
            evacuate(q, *spots("b%d" % b, code), k + b)

        def their_steps():
            for k, src, region, bias in ((2, cols("kf", 10, 20), ("kf", 10, 20), LIFT), (1, T.pk[:], ("pk", 0, 10), col(CN))):
                view, out = lane("pd", 0, k)
                line(view, src, 1.0 / UNIT, bias, [region, ("col", CN, CN + 1)], [out])

        theirs = [steps[1], lambda: apart("kf", "pk")] if ahead else []
        later = [lambda: choose("pr", "pd", 0, 30, T.msp[:], ("msp", 0, 30)),
                 lambda: ts(cols(npl, 10, 20), T.pr[:, 2:30:3], -LIFT, float(UNIT), op.add, op.mult, [("pr", 0, 30)], [(npl, 10, 20)])] if ahead else []

        def lower_layer():
            quant("qz", "qzs", "z", H, H, H)
            layer(0, LO)

        def upper_layer():
            quant("qz", "qzs", "z", 0, H)
            layer(4, UP)

        def upper_codes():
            quant("qu", "qus", "a", 0, H)
            away = topo.chip(core) != topo.chip(partner)
            for far, b in sorted([(far, b) for far in (0, 1) for b in range(4)], key=lambda e: e if away else e[::-1]):
                product(b if far else 4 + b, "eq", "eqs", 128 * b, *((pl, pls) if far else ("qu", "qus")), 0, H)

        def fill(calls):
            for c in calls.split():
                if c[0] == "z": total(UP, int(c[1]), *{"": (0, 10), "a": (0, 4), "b": (4, 10)}[c[2:]])
                elif c[0] == "y": total(LO, int(c[1]))
                elif c[0] == "l": made(c[2], int(c[1]), 0, LO)
                elif c[0] == "u": made(c[2], int(c[1]), 4, UP)
                elif c[0] == "o": unpacked(c[2], int(c[1]), 4, OWN)
                elif c[0] == "f": unpacked(c[2], int(c[1]), 0, FAR)
                elif c[0] == "p": pick(c[1], "su", 0, "gw", WIN, npl, 10)
                else: {"Y": lower_layer, "A": low_codes, "Z": upper_layer, "B": upper_codes, "S": lambda: scan("ssu", "su", H), "E": lambda: entries("stu", "ssu", H)}[c]()

        JUMPS, FILL = AWAY if topo.chip(core) != topo.chip(partner) else HOME
        for c in FILL["sums"].split():
            fill(c)
            if theirs: theirs.pop(0)()
        while theirs: theirs.pop(0)()

        pick("s", "wa", 0, "gw", WIN, npl, 0)
        if ahead: their_steps()
        if HALF: pick("s", "gw", TOP, "wa", WIN, nl, 10)
        fill(FILL["first"])
        win, nxt, power, lists = "wa", "wb", 1, {}
        for k, (by, share, behind_pick, behind_scan, behind_list) in enumerate(JUMPS):
            def step(q, c, d): pick(q, nxt, 16 * c, win, CODES, lists[by], c, d - c)
            fresh = power in [j[0] for j in JUMPS]
            if k: step("s", share, 10)
            elif HALF: pick("s", nxt, 0, "gw", WIN, npl, 0)
            fill(behind_pick)
            scn, lu = "scn%d" % (k % 4), "lu%d" % (k % 4)
            if fresh: scan(scn, win, H)
            if share and k: step("v", 0, share)
            fill(behind_scan)
            if fresh:
                entries(lu, scn, H)
                lists[power] = lu
            if k == 0 and not HALF:
                step("s", share, 10)
                if share: step("v", 0, share)
            if later: later.pop(0)()
            fill(behind_list)
            win, nxt, power = nxt, win, power + by
        pick("v", "cf", 0, win, WIN, nl, 0)
        pick("s", "cf", H, win, CODES, "stu", 0)
        fill(FILL["ends"])
        scan("csc", "cf", C)
        if r == 1: quant("vq", "vqs", "vt", 0, 128)
        fill(FILL["scan"])
        entries("zo", "csc", C)
        fill(FILL["list"])

        def renew(part, b):
            bb = "b%d" % b
            lo, hi = part
            tt(T[xn][:, 4 * lo + b:4 * hi:4], T[bb][:, 0:CODES].indirect(T.zo[:, lo // 16:hi // 16]), T[x][:, 4 * lo + b:4 * hi:4], op.add,
               [(bb, 0, CODES), ("zo", lo // 16, hi // 16), (x, lo, hi, b)], [(xn, lo, hi, b)])

        if r == 0:
            for k, scale in ((S_OWN, 1.0 / (OWN[1] * UNIT)), (S_CUT, -16.0), (S_FAR, 1.0 / (FAR[1] * UNIT))):
                scopy(col(k), col(INV), [("col", INV, INV + 1)], [("col", k, k + 1)], scale)
        if not last:
            for k, (s, b) in enumerate(((S_OWN, LIFT - OWN[0] / (OWN[1] * UNIT)), (S_CUT, 16.0 * (FAR[0] - 6)), (S_FAR, LIFT - FAR[0] / (FAR[1] * UNIT)))):
                line(cols("ka", 20 * k, 20 * k + 20), T.csc[:, 15:C:16], col(s), b, [("csc", 0, C), ("col", s, s + 1)], [("ka", 20 * k, 20 * k + 20)])
        else:
            for code, first_column in ((OWN, 0.0), (FAR, float(H))):
                view, region = spots("fin", code)
                line(view, T.ident[:], 1.0, first_column, [("ident", 0, H)], [region])
            pick("s", "mof", 0, "fin", CODES, "zo", 0, 20)
        for b in range(4):
            renew(P1 if b >= WHOLE else (0, C), b)
            if not last: plane(xn, b, LO)
        renew(P2, WHOLE)
        state_quant(xn, P1)
        if not last:
            scores(P1)
            scores_low_out()
        else: scores(P1, "vq", "vqs")
        for b in range(WHOLE + 1, 4):
            renew(P2, b)
        if not last:
            tt(T.kf[:], cols("ka", 0, 20), cols("ka", 20, 40), op.min, [("ka", 0, 40)], [("kf", 0, 20)])
        state_quant(xn, P2)
        if not last:
            scores(P2)
            tt(T.kb[:], T.kf[:], cols("ka", 40, 60), op.max, [("kf", 0, 20), ("ka", 40, 60)], [("kb", 0, 20)])
            compare(r + 1, P1)
            apart("kb", "dk")
            for b in range(4):
                plane(xn, b, UP)
                if b == 1: lower_places()
        else: scores(P2, "vq", "vqs")

    def store(q, out, in_, region):
        do(q, lambda e: e.dma_start(out, in_), [region], [], "outs")

    store("y", T.mo[:], T.mof[0:128:16, :], ("mof", 0, C))
    for (lo, hi), bank in ((P1, 0), (P2, 4)):
        store("y", T.oc[:, 4 * lo:4 * hi], cols("qx", lo, hi).bitcast(dt.uint8), ("qx", lo, hi))
        evacuate("s", cols("yb", lo, hi), ("yb", lo, hi), bank, 1.0, 0, hi - lo)
        store("s", T.y[:, lo:hi], cols("yb", lo, hi), ("yb", lo, hi))
    for k in range(4):
        store("y", T.osc[4 * k:4 * k + 4, :], T.qxs[32 * k:32 * k + 4, 0:C], ("qxs", 0, C))
    for s in SEMAPHORES:
        if count.get(s, 0): g.wait_ge(T.sem[s], count[s])
